import numpy as np
import ml_dtypes


def mxq(x, axis, fmt="e4m3"):
    dtype, down = {"e4m3": (ml_dtypes.float8_e4m3fn, 7), "e5m2": (ml_dtypes.float8_e5m2, 14)}[fmt]
    v = np.moveaxis(np.asarray(x, np.float32).astype(ml_dtypes.bfloat16).astype(np.float64), axis, -1)
    blocks = v.reshape(v.shape[:-1] + (-1, 32))
    amax = np.abs(blocks).max(-1, keepdims=True)
    byte = np.maximum(np.where(amax > 0, np.frexp(amax)[1] - 1 + 127, 0) - down, 1)
    scale = np.exp2(byte - 127.0)
    codes = (blocks / scale).astype(np.float32).astype(dtype).astype(np.float64)
    return np.moveaxis((codes * scale).reshape(v.shape), -1, axis)


WIDE = False


def mx_kscale(k):
    if not WIDE:
        return np.ones(k)
    levels = np.array([24, -24, 12, -12, 0])
    if k % 512:
        return np.exp2(np.random.permutation(np.resize(levels, k // 32))).repeat(32)
    a = np.empty((k // 512, 16))
    for p in range(k // 512):
        a[p, :8] = np.random.permutation(np.resize(levels, 8))
        for g in range(8):
            far = levels[np.abs(levels - a[p, g]) >= 10]
            a[p, g + 8] = far[np.random.randint(len(far))]
    return np.exp2(a.ravel()).repeat(32)


def f64(x):
    return np.asarray(x).astype(np.float64)


E2M1 = np.array([0.0, 0.5, 1.0, 1.5, 2.0, 3.0, 4.0, 6.0, -0.0, -0.5, -1.0, -1.5, -2.0, -3.0, -4.0, -6.0])


def pack_weight(w, fmt):
    k, n = w.shape
    w = f64(np.asarray(w, np.float32).astype(ml_dtypes.bfloat16)).reshape(k // 32, 32, n)
    amax = np.abs(w).max(1)
    if fmt == "e4m3":
        byte = np.frexp(amax)[1] - 1 + 127 - 7
    else:
        mant, ex = np.frexp(amax / 6.0)
        byte = np.where(mant > 0.5, ex, ex - 1) + 127
    byte = np.clip(np.where(amax > 0, byte, 1), 1, 254)
    scaled = (w * np.exp2(127.0 - byte)[:, None, :]).reshape(k, n).astype(np.float32)
    by_word = np.ascontiguousarray(scaled.reshape(k // 512, 128, 4, n).transpose(0, 1, 3, 2))
    if fmt == "e4m3":
        words = by_word.astype(ml_dtypes.float8_e4m3fn).view(np.uint8)
    else:
        c = by_word.astype(ml_dtypes.float4_e2m1fn).view(np.uint8) & 0xF
        words = (c[..., 0::2] | (c[..., 1::2] << 4)).reshape(k // 512, 128, 2 * n)
    return np.ascontiguousarray(words), np.ascontiguousarray(byte.astype(np.uint8).reshape(k // 512, 16, n))


def unpack_weight(words, scales, fmt):
    g, _, n = scales.shape
    words = np.ascontiguousarray(words).reshape(g, 128, n, -1)
    if fmt == "e4m3":
        vals = words.view(ml_dtypes.float8_e4m3fn).astype(np.float64)
    else:
        nib = np.empty((g, 128, n, 4), np.uint8)
        nib[..., 0::2] = words & 0xF
        nib[..., 1::2] = words >> 4
        vals = E2M1[nib]
    vals = vals * np.repeat(np.exp2(scales.astype(np.float64) - 127.0), 8, axis=1)[..., None]
    return vals.transpose(0, 1, 3, 2).reshape(g * 512, n)


def planes(y):
    n, m = y.shape
    v = y.astype(np.float32).astype(ml_dtypes.bfloat16).astype(np.float64).reshape(n // 32, 32, m)
    top = np.abs(v).max(1)
    byte = np.clip(np.where(top > 0, np.frexp(top)[1] - 1 + 127 - 7, 1), 1, 254)
    codes = (v * np.exp2(127.0 - byte)[:, None, :]).reshape(n, m).astype(np.float32).astype(ml_dtypes.float8_e4m3fn).view(np.uint8)
    words = codes.reshape(n // 512, 128, 4, m).transpose(0, 1, 3, 2)
    return np.ascontiguousarray(words), np.ascontiguousarray(byte.astype(np.uint8).reshape(n // 512, 16, m))


K, D, M, J = 512, 1024, 512, 512


def setup_inputs():
    n = np.random.standard_normal
    u = mx_kscale(D)[:, None]
    s3 = mx_kscale(K)[:, None]
    s = mx_kscale(K)[:, None]
    p_wk = pack_weight(n((K, D)) / np.sqrt(K) / s3 * u.T, "e2m1")
    return {
        "x": (n((K, M)) * s).astype(np.float32),
        "w": (n((K, D)) / np.sqrt(K) / s / u.T).astype(np.float32),
        "c": (n((K, J)) * s3).astype(np.float32),
        "wk_words": p_wk[0],
        "wk_scales": p_wk[1],
        "msk": (np.where(np.random.rand(M, J) < 0.2, -4.0, 0.0)).astype(np.float32),
    }


def reference(x, w, c, wk_words, wk_scales, msk):
    x_ = mxq(f64(x), 0, "e4m3")
    w_ = mxq(f64(w), 0, "e4m3")
    qr = w_.T @ x_
    qr_ = mxq(qr, 0, "e4m3")
    c_ = mxq(f64(c), 0, "e4m3")
    wk_ = unpack_weight(wk_words, wk_scales, "e2m1")
    kc = wk_.T @ c_
    kc_ = mxq(kc, 0, "e4m3")
    sc = qr_.T @ kc_
    return (sc * 0.03125 + f64(msk), kc) + planes(kc)

@@ -1,0 +1,244 @@
+from contextlib import ExitStack
+
+import concourse.mybir as mybir
+
+K, D, M, J = 512, 1024, 512, 512
+FLOPS = 2 * K * D * M + 2 * K * D * J + 2 * D * M * J
+
+F32 = mybir.dt.float32
+BF16 = mybir.dt.bfloat16
+I32 = mybir.dt.int32
+U32 = mybir.dt.uint32
+U8 = mybir.dt.uint8
+FP8X4 = mybir.dt.float8_e4m3fn_x4
+FP4X4 = mybir.dt.float4_e2m1fn_x4
+ALU = mybir.AluOpType
+
+P = 128
+PACK = 4
+SPAN = P * PACK
+D_PASSES = D // SPAN
+SCORE_SCALE = 0.03125
+HALF = SPAN // 2
+
+
+def tile_mix_kvw_mask_kernel(tc, x, w, c, wk_words, wk_scales, msk, out_0, out_1, out_2, out_3):
+    nc = tc.nc
+
+    with ExitStack() as ctx:
+        sb = ctx.enter_context(tc.tile_pool(name="sb", bufs=1))
+        psum = ctx.enter_context(tc.psum_pool(name="psum", bufs=1))
+        ctx.enter_context(tc.manual_schedule())
+
+        def new_tile(name, shape, dtype):
+            return sb.tile(shape, dtype, name=name, align_bytes=64)
+
+        def bank(number, name):
+            return psum.tile([P, SPAN], F32, tag="bank%d" % number, name=name)
+
+        def copy(engine, out, in_):
+            if engine == "vector":
+                nc.vector.tensor_copy(out=out, in_=in_)
+            else:
+                nc.scalar.copy(out=out, in_=in_)
+
+        def round_side_by_side(engine, staged, raw, cols):
+            out = staged[:, cols, :].rearrange("p (g i) t -> p g t i", i=PACK)
+            in_ = raw[:, :, cols].rearrange("p t (g i) -> p g t i", i=PACK)
+            copy(engine, out, in_)
+
+        def round_dealt(engine, staged, raw, half):
+            rs = slice(2 * half, 2 * half + 2)
+            out = staged[:].rearrange("p (r n) t -> p n t r", r=PACK)[:, :, :, rs]
+            in_ = raw[:].rearrange("p t (n r) -> p n t r", r=PACK)[:, :, :, rs]
+            copy(engine, out, in_)
+
+        def quantize(codes, scales, staged, cols):
+            nc.vector.quantize_mx(
+                out=codes[:, cols].bitcast(FP8X4),
+                scales=scales[:, cols],
+                in_=staged[:, cols, :].rearrange("p n t -> p (n t)"),
+            )
+
+        halves = [slice(0, HALF), slice(HALF, SPAN)]
+        whole = slice(0, SPAN)
+
+        wk_raw = new_tile("wk_raw", [P, 2 * D], U8)
+        wks_raw = new_tile("wks_raw", [P, D], U8)
+        wk_codes = new_tile("wk_codes", [P, 2 * D], U8)
+        wk_planes = new_tile("wk_planes", [P, D], U8)
+        c_raw = new_tile("c_raw", [P, PACK, J], F32)
+        x_raw = new_tile("x_raw", [P, PACK, M], F32)
+        w_raw = [new_tile("w_raw%d" % a, [P, PACK, SPAN], F32) for a in range(D_PASSES)]
+        mask = new_tile("mask", [P, PACK, J], F32)
+        c_bf = new_tile("c_bf", [P, J, PACK], BF16)
+        x_bf = new_tile("x_bf", [P, M, PACK], BF16)
+        w_bf = [new_tile("w_bf%d" % a, [P, SPAN, PACK], BF16) for a in range(D_PASSES)]
+        k_bf = [new_tile("k_bf%d" % a, [P, J, PACK], BF16) for a in range(D_PASSES)]
+        q_bf = [new_tile("q_bf%d" % a, [P, M, PACK], BF16) for a in range(D_PASSES)]
+        k_f32 = [new_tile("k_f32%d" % a, [P, PACK, J], F32) for a in range(D_PASSES)]
+        c_codes = new_tile("c_codes", [P, J], U32)
+        c_scales = new_tile("c_scales", [P, J], U8)
+        x_codes = new_tile("x_codes", [P, M], U32)
+        x_scales = new_tile("x_scales", [P, M], U8)
+        w_codes = [new_tile("w_codes%d" % a, [P, SPAN], U32) for a in range(D_PASSES)]
+        w_scales = [new_tile("w_scales%d" % a, [P, SPAN], U8) for a in range(D_PASSES)]
+        q_codes = [new_tile("q_codes%d" % a, [P, M], U32) for a in range(D_PASSES)]
+        q_scales = [new_tile("q_scales%d" % a, [P, M], U8) for a in range(D_PASSES)]
+        k_codes = new_tile("k_codes", [P, D_PASSES, J], U32)
+        k_scales = new_tile("k_scales", [P, D_PASSES, J], U8)
+        scores = new_tile("scores", [P, PACK, J], F32)
+
+        nc.vector.memset(wks_raw[:].bitcast(I32), 0)
+        nc.sync.dma_start(out=wk_raw[:].bitcast(I32), in_=wk_words[0].bitcast(I32))
+        for quad in range(4):
+            nc.scalar.dma_start(
+                out=wks_raw[32 * quad : 32 * quad + 4, :].bitcast(I32),
+                in_=wk_scales[0, 4 * quad : 4 * quad + 4, :].bitcast(I32),
+            )
+        nc.sync.dma_start(out=c_raw[:], in_=c.rearrange("(p t) j -> p t j", t=PACK))
+        nc.sync.dma_start(out=x_raw[:], in_=x.rearrange("(p t) m -> p t m", t=PACK))
+        for a in range(D_PASSES):
+            nc.sync.dma_start(
+                out=w_raw[a][:],
+                in_=w[:, a * SPAN : (a + 1) * SPAN].rearrange("(p t) d -> p t d", t=PACK),
+            )
+
+        for a in range(D_PASSES):
+            cols = slice(2 * SPAN * a, 2 * SPAN * (a + 1))
+            nc.vector.tensor_copy(
+                out=wk_codes[:, cols].rearrange("p (r n b) -> p n r b", r=PACK, b=2),
+                in_=wk_raw[:, cols].rearrange("p (n r b) -> p n r b", r=PACK, b=2),
+            )
+        nc.vector.tensor_copy(
+            out=wk_planes[:].rearrange("p (a r n) -> p a n r", a=D_PASSES, r=PACK),
+            in_=wks_raw[:].rearrange("p (a n r) -> p a n r", a=D_PASSES, r=PACK),
+        )
+
+        round_side_by_side("scalar", c_bf, c_raw, slice(384, 512))
+        round_side_by_side("vector", c_bf, c_raw, slice(0, 256))
+        round_side_by_side("vector", c_bf, c_raw, slice(256, 384))
+        for cols in halves:
+            quantize(c_codes, c_scales, c_bf, cols)
+
+        def keys(a):
+            for r in range(PACK):
+                acc = bank(PACK * a + r, "k_acc")
+                col = SPAN * a + P * r
+                nc.tensor.matmul_mx(
+                    out=acc[:],
+                    lhsT=wk_codes[:, 2 * col : 2 * (col + P)].bitcast(FP4X4),
+                    lhsT_scale=wk_planes[:, col : col + P],
+                    rhs=c_codes[:].bitcast(FP8X4),
+                    rhs_scale=c_scales[:],
+                    start=True,
+                    stop=True,
+                )
+                nc.scalar.copy(out=k_f32[a][:, r, :], in_=acc[:])
+
+        def queries(a):
+            for s in range(PACK):
+                acc = bank(PACK * a + s, "q_acc")
+                ms = slice(P * s, P * (s + 1))
+                for r in range(PACK):
+                    rs = slice(P * r, P * (r + 1))
+                    nc.tensor.matmul_mx(
+                        out=acc[:, rs],
+                        lhsT=w_codes[a][:, rs].bitcast(FP8X4),
+                        lhsT_scale=w_scales[a][:, rs],
+                        rhs=x_codes[:, ms].bitcast(FP8X4),
+                        rhs_scale=x_scales[:, ms],
+                        start=True,
+                        stop=True,
+                    )
+                nc.scalar.copy(out=q_bf[a][:, ms, :], in_=acc[:].rearrange("p (r n) -> p n r", r=PACK))
+
+        def store_keys(a):
+            nc.sync.dma_start(
+                out=out_1[a * SPAN : (a + 1) * SPAN, :].rearrange("(p r) j -> p r j", r=PACK),
+                in_=k_f32[a][:],
+            )
+
+        def quantize_keys(a):
+            nc.vector.quantize_mx(
+                out=k_codes[:, a, :].bitcast(FP8X4),
+                scales=k_scales[:, a, :],
+                in_=k_bf[a][:].rearrange("p n t -> p (n t)"),
+            )
+
+        def score_pass(acc, s, a):
+            ms = slice(P * s, P * (s + 1))
+            nc.tensor.matmul_mx(
+                out=acc[:],
+                lhsT=q_codes[a][:, ms].bitcast(FP8X4),
+                lhsT_scale=q_scales[a][:, ms],
+                rhs=k_codes[:, a, :].bitcast(FP8X4),
+                rhs_scale=k_scales[:, a, :],
+                start=(a == 0),
+                stop=(a == D_PASSES - 1),
+            )
+
+        keys(0)
+        store_keys(0)
+        nc.sync.dma_start(out=mask[:], in_=msk.rearrange("(p s) j -> p s j", s=PACK))
+        keys(1)
+        store_keys(1)
+
+        for half in range(2):
+            round_dealt("vector", x_bf, x_raw, half)
+        for cols in halves:
+            quantize(x_codes, x_scales, x_bf, cols)
+        for half in range(2):
+            round_dealt("vector", w_bf[0], w_raw[0], half)
+        for cols in halves:
+            quantize(w_codes[0], w_scales[0], w_bf[0], cols)
+
+        round_dealt("scalar", w_bf[1], w_raw[1], 1)
+        queries(0)
+        round_side_by_side("vector", k_bf[0], k_f32[0], whole)
+        round_dealt("vector", w_bf[1], w_raw[1], 0)
+        quantize_keys(0)
+        quantize(w_codes[1], w_scales[1], w_bf[1], whole)
+        queries(1)
+        round_side_by_side("vector", k_bf[1], k_f32[1], whole)
+        quantize(q_codes[0], q_scales[0], q_bf[0], whole)
+        quantize_keys(1)
+
+        nc.sync.dma_start(
+            out=out_2.rearrange("a p j i -> p a (j i)").bitcast(I32),
+            in_=k_codes[:].bitcast(I32),
+        )
+        for quad in range(4):
+            nc.sync.dma_start(
+                out=out_3[:, 4 * quad : 4 * quad + 4, :].rearrange("a q j -> q a j").bitcast(I32),
+                in_=k_scales[32 * quad : 32 * quad + 4, :, :].bitcast(I32),
+            )
+
+        accs = []
+        for s in range(PACK):
+            acc = bank(s, "s_acc")
+            accs.append(acc)
+            score_pass(acc, s, 0)
+
+        rows = out_0.rearrange("(p s) j -> p s j", s=PACK)
+
+        def finish(s):
+            nc.vector.scalar_tensor_tensor(
+                out=scores[:, s, :],
+                in0=accs[s][:],
+                scalar=SCORE_SCALE,
+                in1=mask[:, s, :],
+                op0=ALU.mult,
+                op1=ALU.add,
+            )
+
+        for s in range(PACK + 1):
+            if s < PACK:
+                quantize(q_codes[1], q_scales[1], q_bf[1], slice(P * s, P * (s + 1)))
+                score_pass(accs[s], s, 1)
+            if s >= 1:
+                finish(s - 1)
+            if s == 2:
+                nc.sync.dma_start(out=rows[:, 0:2, :], in_=scores[:, 0:2, :])
+            if s > 2:
+                nc.sync.dma_start(out=rows[:, s - 1, :], in_=scores[:, s - 1, :])

@@ -92,7 +92,7 @@ def tile_mix_kvw_mask_kernel(tc, x, w, c, wk_words, wk_scales, msk, out_0, out_1
         nc.vector.memset(wks_raw[:].bitcast(I32), 0)
         nc.sync.dma_start(out=wk_raw[:].bitcast(I32), in_=wk_words[0].bitcast(I32))
         for quad in range(4):
-            nc.scalar.dma_start(
+            nc.sync.dma_start(
                 out=wks_raw[32 * quad : 32 * quad + 4, :].bitcast(I32),
                 in_=wk_scales[0, 4 * quad : 4 * quad + 4, :].bitcast(I32),
             )
@@ -115,9 +115,9 @@ def tile_mix_kvw_mask_kernel(tc, x, w, c, wk_words, wk_scales, msk, out_0, out_1
             in_=wks_raw[:].rearrange("p (a n r) -> p a n r", a=D_PASSES, r=PACK),
         )
 
-        round_side_by_side("scalar", c_bf, c_raw, slice(384, 512))
-        round_side_by_side("vector", c_bf, c_raw, slice(0, 256))
-        round_side_by_side("vector", c_bf, c_raw, slice(256, 384))
+        for cols in halves:
+            round_side_by_side("vector", c_bf, c_raw, slice(cols.start, cols.start + 160))
+            round_side_by_side("scalar", c_bf, c_raw, slice(cols.start + 160, cols.stop))
         for cols in halves:
             quantize(c_codes, c_scales, c_bf, cols)
 
@@ -135,6 +135,26 @@ def tile_mix_kvw_mask_kernel(tc, x, w, c, wk_words, wk_scales, msk, out_0, out_1
                     stop=True,
                 )
                 nc.scalar.copy(out=k_f32[a][:, r, :], in_=acc[:])
+
+        def keys_by_halves(a):
+            for half, js in enumerate(halves):
+                for pair in range(2):
+                    acc = bank(PACK * a + 2 * half + pair, "k_acc")
+                    for i in range(2):
+                        col = SPAN * a + P * (2 * pair + i)
+                        nc.tensor.matmul_mx(
+                            out=acc[:, halves[i]],
+                            lhsT=wk_codes[:, 2 * col : 2 * (col + P)].bitcast(FP4X4),
+                            lhsT_scale=wk_planes[:, col : col + P],
+                            rhs=c_codes[:, js].bitcast(FP8X4),
+                            rhs_scale=c_scales[:, js],
+                            start=True,
+                            stop=True,
+                        )
+                    nc.scalar.copy(
+                        out=k_f32[a][:, 2 * pair : 2 * pair + 2, js],
+                        in_=acc[:].rearrange("p (i j) -> p i j", i=2),
+                    )
 
         def queries(a):
             for s in range(PACK):
@@ -178,7 +198,7 @@ def tile_mix_kvw_mask_kernel(tc, x, w, c, wk_words, wk_scales, msk, out_0, out_1
                 stop=(a == D_PASSES - 1),
             )
 
-        keys(0)
+        keys_by_halves(0)
         store_keys(0)
         nc.sync.dma_start(out=mask[:], in_=msk.rearrange("(p s) j -> p s j", s=PACK))
         keys(1)
@@ -215,11 +235,6 @@ def tile_mix_kvw_mask_kernel(tc, x, w, c, wk_words, wk_scales, msk, out_0, out_1
             )
 
         accs = []
-        for s in range(PACK):
-            acc = bank(s, "s_acc")
-            accs.append(acc)
-            score_pass(acc, s, 0)
-
         rows = out_0.rearrange("(p s) j -> p s j", s=PACK)
 
         def finish(s):
@@ -235,10 +250,10 @@ def tile_mix_kvw_mask_kernel(tc, x, w, c, wk_words, wk_scales, msk, out_0, out_1
         for s in range(PACK + 1):
             if s < PACK:
                 quantize(q_codes[1], q_scales[1], q_bf[1], slice(P * s, P * (s + 1)))
-                score_pass(accs[s], s, 1)
+                acc = bank(s, "s_acc")
+                accs.append(acc)
+                for a in range(D_PASSES):
+                    score_pass(acc, s, a)
             if s >= 1:
                 finish(s - 1)
-            if s == 2:
-                nc.sync.dma_start(out=rows[:, 0:2, :], in_=scores[:, 0:2, :])
-            if s > 2:
                 nc.sync.dma_start(out=rows[:, s - 1, :], in_=scores[:, s - 1, :])

@@ -85,7 +85,7 @@ def tile_mix_kvw_mask_kernel(tc, x, w, c, wk_words, wk_scales, msk, out_0, out_1
         w_scales = [new_tile("w_scales%d" % a, [P, SPAN], U8) for a in range(D_PASSES)]
         q_codes = [new_tile("q_codes%d" % a, [P, M], U32) for a in range(D_PASSES)]
         q_scales = [new_tile("q_scales%d" % a, [P, M], U8) for a in range(D_PASSES)]
-        k_codes = new_tile("k_codes", [P, D_PASSES, J], U32)
+        k_codes = [new_tile("k_codes%d" % a, [P, J], U32) for a in range(D_PASSES)]
         k_scales = new_tile("k_scales", [P, D_PASSES, J], U8)
         scores = new_tile("scores", [P, PACK, J], F32)
 
@@ -107,12 +107,12 @@ def tile_mix_kvw_mask_kernel(tc, x, w, c, wk_words, wk_scales, msk, out_0, out_1
         for a in range(D_PASSES):
             cols = slice(2 * SPAN * a, 2 * SPAN * (a + 1))
             nc.vector.tensor_copy(
-                out=wk_codes[:, cols].rearrange("p (r n b) -> p n r b", r=PACK, b=2),
-                in_=wk_raw[:, cols].rearrange("p (n r b) -> p n r b", r=PACK, b=2),
+                out=wk_codes[:, cols].rearrange("p (r n b) -> p r n b", r=PACK, b=2),
+                in_=wk_raw[:, cols].rearrange("p (n r b) -> p r n b", r=PACK, b=2),
             )
         nc.vector.tensor_copy(
-            out=wk_planes[:].rearrange("p (a r n) -> p a n r", a=D_PASSES, r=PACK),
-            in_=wks_raw[:].rearrange("p (a n r) -> p a n r", a=D_PASSES, r=PACK),
+            out=wk_planes[:].rearrange("p (a r n) -> p a r n", a=D_PASSES, r=PACK),
+            in_=wks_raw[:].rearrange("p (a n r) -> p a r n", a=D_PASSES, r=PACK),
         )
 
         for cols in halves:
@@ -181,9 +181,15 @@ def tile_mix_kvw_mask_kernel(tc, x, w, c, wk_words, wk_scales, msk, out_0, out_1
 
         def quantize_keys(a):
             nc.vector.quantize_mx(
-                out=k_codes[:, a, :].bitcast(FP8X4),
+                out=k_codes[a][:].bitcast(FP8X4),
                 scales=k_scales[:, a, :],
                 in_=k_bf[a][:].rearrange("p n t -> p (n t)"),
+            )
+
+        def store_key_codes(a):
+            nc.sync.dma_start(
+                out=out_2[a].rearrange("p j i -> p (j i)").bitcast(I32),
+                in_=k_codes[a][:].bitcast(I32),
             )
 
         def score_pass(acc, s, a):
@@ -192,7 +198,7 @@ def tile_mix_kvw_mask_kernel(tc, x, w, c, wk_words, wk_scales, msk, out_0, out_1
                 out=acc[:],
                 lhsT=q_codes[a][:, ms].bitcast(FP8X4),
                 lhsT_scale=q_scales[a][:, ms],
-                rhs=k_codes[:, a, :].bitcast(FP8X4),
+                rhs=k_codes[a][:].bitcast(FP8X4),
                 rhs_scale=k_scales[:, a, :],
                 start=(a == 0),
                 stop=(a == D_PASSES - 1),
@@ -213,28 +219,31 @@ def tile_mix_kvw_mask_kernel(tc, x, w, c, wk_words, wk_scales, msk, out_0, out_1
         for cols in halves:
             quantize(w_codes[0], w_scales[0], w_bf[0], cols)
 
+        round_side_by_side("scalar", k_bf[0], k_f32[0], slice(384, 512))
         round_dealt("scalar", w_bf[1], w_raw[1], 1)
         queries(0)
-        round_side_by_side("vector", k_bf[0], k_f32[0], whole)
+        round_side_by_side("vector", k_bf[0], k_f32[0], slice(0, 384))
         round_dealt("vector", w_bf[1], w_raw[1], 0)
         quantize_keys(0)
+        store_key_codes(0)
         quantize(w_codes[1], w_scales[1], w_bf[1], whole)
         queries(1)
         round_side_by_side("vector", k_bf[1], k_f32[1], whole)
-        quantize(q_codes[0], q_scales[0], q_bf[0], whole)
+        accs = []
+        for s in range(PACK):
+            acc = bank(s, "s_acc")
+            accs.append(acc)
+        quantize(q_codes[0], q_scales[0], q_bf[0], halves[0])
+        score_pass(accs[0], 0, 0)
+        score_pass(accs[1], 1, 0)
         quantize_keys(1)
-
-        nc.sync.dma_start(
-            out=out_2.rearrange("a p j i -> p a (j i)").bitcast(I32),
-            in_=k_codes[:].bitcast(I32),
-        )
+        store_key_codes(1)
         for quad in range(4):
             nc.sync.dma_start(
                 out=out_3[:, 4 * quad : 4 * quad + 4, :].rearrange("a q j -> q a j").bitcast(I32),
                 in_=k_scales[32 * quad : 32 * quad + 4, :, :].bitcast(I32),
             )
 
-        accs = []
         rows = out_0.rearrange("(p s) j -> p s j", s=PACK)
 
         def finish(s):
@@ -250,10 +259,11 @@ def tile_mix_kvw_mask_kernel(tc, x, w, c, wk_words, wk_scales, msk, out_0, out_1
         for s in range(PACK + 1):
             if s < PACK:
                 quantize(q_codes[1], q_scales[1], q_bf[1], slice(P * s, P * (s + 1)))
-                acc = bank(s, "s_acc")
-                accs.append(acc)
-                for a in range(D_PASSES):
-                    score_pass(acc, s, a)
+                score_pass(accs[s], s, 1)
+            if s == 0:
+                quantize(q_codes[0], q_scales[0], q_bf[0], halves[1])
+            if s < 2:
+                score_pass(accs[s + 2], s + 2, 0)
             if s >= 1:
                 finish(s - 1)
                 nc.sync.dma_start(out=rows[:, s - 1, :], in_=scores[:, s - 1, :])

@@ -17,13 +17,21 @@ ALU = mybir.AluOpType
 P = 128
 PACK = 4
 SPAN = P * PACK
-D_PASSES = D // SPAN
-SCORE_SCALE = 0.03125
 HALF = SPAN // 2
+D_SPANS = D // SPAN
+QUADRANTS = 4
+FP4_BYTES = 2
+SCORE_SCALE = 0.03125
+
+C_VECTOR_COLS = 160
+KEYS_EARLY_END = 192
+KEYS_SCALAR_START = 448
 
 
 def tile_mix_kvw_mask_kernel(tc, x, w, c, wk_words, wk_scales, msk, out_0, out_1, out_2, out_3):
     nc = tc.nc
+    halves = [slice(0, HALF), slice(HALF, SPAN)]
+    whole = slice(0, SPAN)
 
     with ExitStack() as ctx:
         sb = ctx.enter_context(tc.tile_pool(name="sb", bufs=1))
@@ -33,25 +41,64 @@ def tile_mix_kvw_mask_kernel(tc, x, w, c, wk_words, wk_scales, msk, out_0, out_1
         def new_tile(name, shape, dtype):
             return sb.tile(shape, dtype, name=name, align_bytes=64)
 
+        def span_tiles(name, shape, dtype):
+            return [new_tile("%s%d" % (name, a), shape, dtype) for a in range(D_SPANS)]
+
         def bank(number, name):
             return psum.tile([P, SPAN], F32, tag="bank%d" % number, name=name)
 
-        def copy(engine, out, in_):
-            if engine == "vector":
-                nc.vector.tensor_copy(out=out, in_=in_)
-            else:
-                nc.scalar.copy(out=out, in_=in_)
+        wk_words_raw = new_tile("wk_words_raw", [P, FP4_BYTES * D], U8)
+        wk_scales_raw = new_tile("wk_scales_raw", [P, D], U8)
+        c_raw = new_tile("c_raw", [P, PACK, J], F32)
+        x_raw = new_tile("x_raw", [P, PACK, M], F32)
+        w_raw = span_tiles("w_raw", [P, PACK, SPAN], F32)
+        mask = new_tile("mask", [P, PACK, J], F32)
+        c_bf = new_tile("c_bf", [P, J, PACK], BF16)
+        x_bf = new_tile("x_bf", [P, M, PACK], BF16)
+        w_bf = span_tiles("w_bf", [P, SPAN, PACK], BF16)
+        k_bf = span_tiles("k_bf", [P, J, PACK], BF16)
+        q_bf = span_tiles("q_bf", [P, M, PACK], BF16)
+        wk_dealt_words = new_tile("wk_dealt_words", [P, FP4_BYTES * D], U8)
+        wk_dealt_scales = new_tile("wk_dealt_scales", [P, D], U8)
+        c_codes = new_tile("c_codes", [P, J], U32)
+        c_scales = new_tile("c_scales", [P, J], U8)
+        x_codes = new_tile("x_codes", [P, M], U32)
+        x_scales = new_tile("x_scales", [P, M], U8)
+        w_codes = span_tiles("w_codes", [P, SPAN], U32)
+        w_scales = span_tiles("w_scales", [P, SPAN], U8)
+        q_codes = span_tiles("q_codes", [P, M], U32)
+        q_scales = span_tiles("q_scales", [P, M], U8)
+        k_codes = span_tiles("k_codes", [P, J], U32)
+        k_scales = new_tile("k_scales", [P, D_SPANS, J], U8)
+        k_f32 = span_tiles("k_f32", [P, PACK, J], F32)
+        scores = new_tile("scores", [P, PACK, J], F32)
 
-        def round_side_by_side(engine, staged, raw, cols):
-            out = staged[:, cols, :].rearrange("p (g i) t -> p g t i", i=PACK)
-            in_ = raw[:, :, cols].rearrange("p t (g i) -> p g t i", i=PACK)
-            copy(engine, out, in_)
+        def deal_wk_words(a):
+            byte_cols = slice(FP4_BYTES * SPAN * a, FP4_BYTES * SPAN * (a + 1))
+            nc.vector.tensor_copy(
+                out=wk_dealt_words[:, byte_cols].rearrange("p (r n b) -> p r n b", r=PACK, b=FP4_BYTES),
+                in_=wk_words_raw[:, byte_cols].rearrange("p (n r b) -> p r n b", r=PACK, b=FP4_BYTES),
+            )
 
-        def round_dealt(engine, staged, raw, half):
-            rs = slice(2 * half, 2 * half + 2)
-            out = staged[:].rearrange("p (r n) t -> p n t r", r=PACK)[:, :, :, rs]
-            in_ = raw[:].rearrange("p t (n r) -> p n t r", r=PACK)[:, :, :, rs]
-            copy(engine, out, in_)
+        def deal_wk_scales(a):
+            cols = slice(SPAN * a, SPAN * (a + 1))
+            nc.vector.tensor_copy(
+                out=wk_dealt_scales[:, cols].rearrange("p (r n) -> p r n", r=PACK),
+                in_=wk_scales_raw[:, cols].rearrange("p (n r) -> p r n", r=PACK),
+            )
+
+        def round_columns(copy, staged, raw, cols):
+            copy(
+                out=staged[:, cols, :].rearrange("p (g i) t -> p g t i", i=PACK),
+                in_=raw[:, :, cols].rearrange("p t (g i) -> p g t i", i=PACK),
+            )
+
+        def round_dealt(copy, staged, raw, half):
+            groups = slice(2 * half, 2 * half + 2)
+            copy(
+                out=staged[:].rearrange("p (r n) t -> p n t r", r=PACK)[:, :, :, groups],
+                in_=raw[:].rearrange("p t (n r) -> p n t r", r=PACK)[:, :, :, groups],
+            )
 
         def quantize(codes, scales, staged, cols):
             nc.vector.quantize_mx(
@@ -60,118 +107,34 @@ def tile_mix_kvw_mask_kernel(tc, x, w, c, wk_words, wk_scales, msk, out_0, out_1
                 in_=staged[:, cols, :].rearrange("p n t -> p (n t)"),
             )
 
-        halves = [slice(0, HALF), slice(HALF, SPAN)]
-        whole = slice(0, SPAN)
-
-        wk_raw = new_tile("wk_raw", [P, 2 * D], U8)
-        wks_raw = new_tile("wks_raw", [P, D], U8)
-        wk_codes = new_tile("wk_codes", [P, 2 * D], U8)
-        wk_planes = new_tile("wk_planes", [P, D], U8)
-        c_raw = new_tile("c_raw", [P, PACK, J], F32)
-        x_raw = new_tile("x_raw", [P, PACK, M], F32)
-        w_raw = [new_tile("w_raw%d" % a, [P, PACK, SPAN], F32) for a in range(D_PASSES)]
-        mask = new_tile("mask", [P, PACK, J], F32)
-        c_bf = new_tile("c_bf", [P, J, PACK], BF16)
-        x_bf = new_tile("x_bf", [P, M, PACK], BF16)
-        w_bf = [new_tile("w_bf%d" % a, [P, SPAN, PACK], BF16) for a in range(D_PASSES)]
-        k_bf = [new_tile("k_bf%d" % a, [P, J, PACK], BF16) for a in range(D_PASSES)]
-        q_bf = [new_tile("q_bf%d" % a, [P, M, PACK], BF16) for a in range(D_PASSES)]
-        k_f32 = [new_tile("k_f32%d" % a, [P, PACK, J], F32) for a in range(D_PASSES)]
-        c_codes = new_tile("c_codes", [P, J], U32)
-        c_scales = new_tile("c_scales", [P, J], U8)
-        x_codes = new_tile("x_codes", [P, M], U32)
-        x_scales = new_tile("x_scales", [P, M], U8)
-        w_codes = [new_tile("w_codes%d" % a, [P, SPAN], U32) for a in range(D_PASSES)]
-        w_scales = [new_tile("w_scales%d" % a, [P, SPAN], U8) for a in range(D_PASSES)]
-        q_codes = [new_tile("q_codes%d" % a, [P, M], U32) for a in range(D_PASSES)]
-        q_scales = [new_tile("q_scales%d" % a, [P, M], U8) for a in range(D_PASSES)]
-        k_codes = [new_tile("k_codes%d" % a, [P, J], U32) for a in range(D_PASSES)]
-        k_scales = new_tile("k_scales", [P, D_PASSES, J], U8)
-        scores = new_tile("scores", [P, PACK, J], F32)
-
-        nc.vector.memset(wks_raw[:].bitcast(I32), 0)
-        nc.sync.dma_start(out=wk_raw[:].bitcast(I32), in_=wk_words[0].bitcast(I32))
-        for quad in range(4):
-            nc.sync.dma_start(
-                out=wks_raw[32 * quad : 32 * quad + 4, :].bitcast(I32),
-                in_=wk_scales[0, 4 * quad : 4 * quad + 4, :].bitcast(I32),
+        def key_pass(out, a, r, js):
+            col = SPAN * a + P * r
+            nc.tensor.matmul_mx(
+                out=out,
+                lhsT=wk_dealt_words[:, FP4_BYTES * col : FP4_BYTES * (col + P)].bitcast(FP4X4),
+                lhsT_scale=wk_dealt_scales[:, col : col + P],
+                rhs=c_codes[:, js].bitcast(FP8X4),
+                rhs_scale=c_scales[:, js],
+                start=True,
+                stop=True,
             )
-        nc.sync.dma_start(out=c_raw[:], in_=c.rearrange("(p t) j -> p t j", t=PACK))
-        nc.sync.dma_start(out=x_raw[:], in_=x.rearrange("(p t) m -> p t m", t=PACK))
-        for a in range(D_PASSES):
-            nc.sync.dma_start(
-                out=w_raw[a][:],
-                in_=w[:, a * SPAN : (a + 1) * SPAN].rearrange("(p t) d -> p t d", t=PACK),
-            )
-
-        for a in range(D_PASSES):
-            cols = slice(2 * SPAN * a, 2 * SPAN * (a + 1))
-            nc.vector.tensor_copy(
-                out=wk_codes[:, cols].rearrange("p (r n b) -> p r n b", r=PACK, b=2),
-                in_=wk_raw[:, cols].rearrange("p (n r b) -> p r n b", r=PACK, b=2),
-            )
-        nc.vector.tensor_copy(
-            out=wk_planes[:].rearrange("p (a r n) -> p a r n", a=D_PASSES, r=PACK),
-            in_=wks_raw[:].rearrange("p (a n r) -> p a r n", a=D_PASSES, r=PACK),
-        )
-
-        for cols in halves:
-            round_side_by_side("vector", c_bf, c_raw, slice(cols.start, cols.start + 160))
-            round_side_by_side("scalar", c_bf, c_raw, slice(cols.start + 160, cols.stop))
-        for cols in halves:
-            quantize(c_codes, c_scales, c_bf, cols)
-
-        def keys(a):
-            for r in range(PACK):
-                acc = bank(PACK * a + r, "k_acc")
-                col = SPAN * a + P * r
-                nc.tensor.matmul_mx(
-                    out=acc[:],
-                    lhsT=wk_codes[:, 2 * col : 2 * (col + P)].bitcast(FP4X4),
-                    lhsT_scale=wk_planes[:, col : col + P],
-                    rhs=c_codes[:].bitcast(FP8X4),
-                    rhs_scale=c_scales[:],
-                    start=True,
-                    stop=True,
-                )
-                nc.scalar.copy(out=k_f32[a][:, r, :], in_=acc[:])
 
         def keys_by_halves(a):
             for half, js in enumerate(halves):
                 for pair in range(2):
                     acc = bank(PACK * a + 2 * half + pair, "k_acc")
                     for i in range(2):
-                        col = SPAN * a + P * (2 * pair + i)
-                        nc.tensor.matmul_mx(
-                            out=acc[:, halves[i]],
-                            lhsT=wk_codes[:, 2 * col : 2 * (col + P)].bitcast(FP4X4),
-                            lhsT_scale=wk_planes[:, col : col + P],
-                            rhs=c_codes[:, js].bitcast(FP8X4),
-                            rhs_scale=c_scales[:, js],
-                            start=True,
-                            stop=True,
-                        )
+                        key_pass(acc[:, halves[i]], a, 2 * pair + i, js)
                     nc.scalar.copy(
                         out=k_f32[a][:, 2 * pair : 2 * pair + 2, js],
                         in_=acc[:].rearrange("p (i j) -> p i j", i=2),
                     )
 
-        def queries(a):
-            for s in range(PACK):
-                acc = bank(PACK * a + s, "q_acc")
-                ms = slice(P * s, P * (s + 1))
-                for r in range(PACK):
-                    rs = slice(P * r, P * (r + 1))
-                    nc.tensor.matmul_mx(
-                        out=acc[:, rs],
-                        lhsT=w_codes[a][:, rs].bitcast(FP8X4),
-                        lhsT_scale=w_scales[a][:, rs],
-                        rhs=x_codes[:, ms].bitcast(FP8X4),
-                        rhs_scale=x_scales[:, ms],
-                        start=True,
-                        stop=True,
-                    )
-                nc.scalar.copy(out=q_bf[a][:, ms, :], in_=acc[:].rearrange("p (r n) -> p n r", r=PACK))
+        def keys_whole(a):
+            for r in range(PACK):
+                acc = bank(PACK * a + r, "k_acc")
+                key_pass(acc[:], a, r, whole)
+                nc.scalar.copy(out=k_f32[a][:, r, :], in_=acc[:])
 
         def store_keys(a):
             nc.sync.dma_start(
@@ -179,91 +142,126 @@ def tile_mix_kvw_mask_kernel(tc, x, w, c, wk_words, wk_scales, msk, out_0, out_1
                 in_=k_f32[a][:],
             )
 
-        def quantize_keys(a):
-            nc.vector.quantize_mx(
-                out=k_codes[a][:].bitcast(FP8X4),
-                scales=k_scales[:, a, :],
-                in_=k_bf[a][:].rearrange("p n t -> p (n t)"),
-            )
-
-        def store_key_codes(a):
+        def quantize_and_store_keys(a):
+            quantize(k_codes[a], k_scales[:, a, :], k_bf[a], whole)
             nc.sync.dma_start(
                 out=out_2[a].rearrange("p j i -> p (j i)").bitcast(I32),
                 in_=k_codes[a][:].bitcast(I32),
             )
 
-        def score_pass(acc, s, a):
+        def queries(a):
+            for s in range(PACK):
+                acc = bank(PACK * a + s, "q_acc")
+                ms = slice(P * s, P * (s + 1))
+                for r in range(PACK):
+                    group = slice(P * r, P * (r + 1))
+                    nc.tensor.matmul_mx(
+                        out=acc[:, group],
+                        lhsT=w_codes[a][:, group].bitcast(FP8X4),
+                        lhsT_scale=w_scales[a][:, group],
+                        rhs=x_codes[:, ms].bitcast(FP8X4),
+                        rhs_scale=x_scales[:, ms],
+                        start=True,
+                        stop=True,
+                    )
+                nc.scalar.copy(out=q_bf[a][:, ms, :], in_=acc[:].rearrange("p (r n) -> p n r", r=PACK))
+
+        def score_pass(s, a):
             ms = slice(P * s, P * (s + 1))
             nc.tensor.matmul_mx(
-                out=acc[:],
+                out=score_acc[s][:],
                 lhsT=q_codes[a][:, ms].bitcast(FP8X4),
                 lhsT_scale=q_scales[a][:, ms],
                 rhs=k_codes[a][:].bitcast(FP8X4),
                 rhs_scale=k_scales[:, a, :],
                 start=(a == 0),
-                stop=(a == D_PASSES - 1),
+                stop=(a == D_SPANS - 1),
             )
 
-        keys_by_halves(0)
-        store_keys(0)
-        nc.sync.dma_start(out=mask[:], in_=msk.rearrange("(p s) j -> p s j", s=PACK))
-        keys(1)
-        store_keys(1)
+        def close_score_tile(s):
+            quantize(q_codes[1], q_scales[1], q_bf[1], slice(P * s, P * (s + 1)))
+            score_pass(s, 1)
 
-        for half in range(2):
-            round_dealt("vector", x_bf, x_raw, half)
-        for cols in halves:
-            quantize(x_codes, x_scales, x_bf, cols)
-        for half in range(2):
-            round_dealt("vector", w_bf[0], w_raw[0], half)
-        for cols in halves:
-            quantize(w_codes[0], w_scales[0], w_bf[0], cols)
-
-        round_side_by_side("scalar", k_bf[0], k_f32[0], slice(384, 512))
-        round_dealt("scalar", w_bf[1], w_raw[1], 1)
-        queries(0)
-        round_side_by_side("vector", k_bf[0], k_f32[0], slice(0, 384))
-        round_dealt("vector", w_bf[1], w_raw[1], 0)
-        quantize_keys(0)
-        store_key_codes(0)
-        quantize(w_codes[1], w_scales[1], w_bf[1], whole)
-        queries(1)
-        round_side_by_side("vector", k_bf[1], k_f32[1], whole)
-        accs = []
-        for s in range(PACK):
-            acc = bank(s, "s_acc")
-            accs.append(acc)
-        quantize(q_codes[0], q_scales[0], q_bf[0], halves[0])
-        score_pass(accs[0], 0, 0)
-        score_pass(accs[1], 1, 0)
-        quantize_keys(1)
-        store_key_codes(1)
-        for quad in range(4):
-            nc.sync.dma_start(
-                out=out_3[:, 4 * quad : 4 * quad + 4, :].rearrange("a q j -> q a j").bitcast(I32),
-                in_=k_scales[32 * quad : 32 * quad + 4, :, :].bitcast(I32),
-            )
-
-        rows = out_0.rearrange("(p s) j -> p s j", s=PACK)
-
-        def finish(s):
+        def finish_score_tile(s):
             nc.vector.scalar_tensor_tensor(
                 out=scores[:, s, :],
-                in0=accs[s][:],
+                in0=score_acc[s][:],
                 scalar=SCORE_SCALE,
                 in1=mask[:, s, :],
                 op0=ALU.mult,
                 op1=ALU.add,
             )
+            nc.sync.dma_start(out=out_0.rearrange("(p s) j -> p s j", s=PACK)[:, s, :], in_=scores[:, s, :])
 
-        for s in range(PACK + 1):
-            if s < PACK:
-                quantize(q_codes[1], q_scales[1], q_bf[1], slice(P * s, P * (s + 1)))
-                score_pass(accs[s], s, 1)
-            if s == 0:
-                quantize(q_codes[0], q_scales[0], q_bf[0], halves[1])
-            if s < 2:
-                score_pass(accs[s + 2], s + 2, 0)
-            if s >= 1:
-                finish(s - 1)
-                nc.sync.dma_start(out=rows[:, s - 1, :], in_=scores[:, s - 1, :])
+        nc.vector.memset(wk_scales_raw[:].bitcast(I32), 0)
+        nc.sync.dma_start(out=wk_words_raw[:].bitcast(I32), in_=wk_words[0].bitcast(I32))
+        for quad in range(QUADRANTS):
+            nc.sync.dma_start(
+                out=wk_scales_raw[32 * quad : 32 * quad + 4, :].bitcast(I32),
+                in_=wk_scales[0, 4 * quad : 4 * quad + 4, :].bitcast(I32),
+            )
+        nc.sync.dma_start(out=c_raw[:], in_=c.rearrange("(p t) j -> p t j", t=PACK))
+        nc.sync.dma_start(out=x_raw[:], in_=x.rearrange("(p t) m -> p t m", t=PACK))
+        for a in range(D_SPANS):
+            nc.sync.dma_start(
+                out=w_raw[a][:],
+                in_=w[:, a * SPAN : (a + 1) * SPAN].rearrange("(p t) d -> p t d", t=PACK),
+            )
+
+        deal_wk_words(0)
+        deal_wk_scales(0)
+        deal_wk_words(1)
+        for cols in halves:
+            round_columns(nc.vector.tensor_copy, c_bf, c_raw, slice(cols.start, cols.start + C_VECTOR_COLS))
+            round_columns(nc.scalar.copy, c_bf, c_raw, slice(cols.start + C_VECTOR_COLS, cols.stop))
+        for cols in halves:
+            quantize(c_codes, c_scales, c_bf, cols)
+        deal_wk_scales(1)
+
+        keys_by_halves(0)
+        store_keys(0)
+        nc.sync.dma_start(out=mask[:], in_=msk.rearrange("(p s) j -> p s j", s=PACK))
+        keys_whole(1)
+        store_keys(1)
+
+        for half in range(2):
+            round_dealt(nc.vector.tensor_copy, x_bf, x_raw, half)
+        for cols in halves:
+            quantize(x_codes, x_scales, x_bf, cols)
+        round_columns(nc.vector.tensor_copy, k_bf[0], k_f32[0], slice(0, KEYS_EARLY_END))
+        for half in range(2):
+            round_dealt(nc.vector.tensor_copy, w_bf[0], w_raw[0], half)
+        for cols in halves:
+            quantize(w_codes[0], w_scales[0], w_bf[0], cols)
+
+        round_columns(nc.scalar.copy, k_bf[0], k_f32[0], slice(KEYS_SCALAR_START, J))
+        round_dealt(nc.scalar.copy, w_bf[1], w_raw[1], 1)
+        queries(0)
+        round_columns(nc.vector.tensor_copy, k_bf[0], k_f32[0], slice(KEYS_EARLY_END, KEYS_SCALAR_START))
+        round_dealt(nc.vector.tensor_copy, w_bf[1], w_raw[1], 0)
+        quantize_and_store_keys(0)
+        quantize(w_codes[1], w_scales[1], w_bf[1], whole)
+        queries(1)
+        round_columns(nc.vector.tensor_copy, k_bf[1], k_f32[1], whole)
+
+        score_acc = [bank(s, "s_acc") for s in range(PACK)]
+        quantize(q_codes[0], q_scales[0], q_bf[0], halves[0])
+        score_pass(0, 0)
+        score_pass(1, 0)
+        quantize_and_store_keys(1)
+        for quad in range(QUADRANTS):
+            nc.sync.dma_start(
+                out=out_3[:, 4 * quad : 4 * quad + 4, :].rearrange("a q j -> q a j").bitcast(I32),
+                in_=k_scales[32 * quad : 32 * quad + 4, :, :].bitcast(I32),
+            )
+
+        close_score_tile(0)
+        quantize(q_codes[0], q_scales[0], q_bf[0], halves[1])
+        score_pass(2, 0)
+        close_score_tile(1)
+        score_pass(3, 0)
+        finish_score_tile(0)
+        for s in range(2, PACK):
+            close_score_tile(s)
+            finish_score_tile(s - 1)
+        finish_score_tile(PACK - 1)

@@ -9,6 +9,7 @@ F32 = mybir.dt.float32
 BF16 = mybir.dt.bfloat16
 I32 = mybir.dt.int32
 U32 = mybir.dt.uint32
+U16 = mybir.dt.uint16
 U8 = mybir.dt.uint8
 FP8X4 = mybir.dt.float8_e4m3fn_x4
 FP4X4 = mybir.dt.float4_e2m1fn_x4
@@ -24,8 +25,10 @@ FP4_BYTES = 2
 SCORE_SCALE = 0.03125
 
 C_VECTOR_COLS = 160
-KEYS_EARLY_END = 192
-KEYS_SCALAR_START = 448
+W1_SPLIT = 40
+KEYS_FIRST_END = 128
+KEYS_SECOND_END = 256
+KEYS_SCALAR_COLS = 224
 
 
 def tile_mix_kvw_mask_kernel(tc, x, w, c, wk_words, wk_scales, msk, out_0, out_1, out_2, out_3):
@@ -49,7 +52,7 @@ def tile_mix_kvw_mask_kernel(tc, x, w, c, wk_words, wk_scales, msk, out_0, out_1
 
         wk_words_raw = new_tile("wk_words_raw", [P, FP4_BYTES * D], U8)
         wk_scales_raw = new_tile("wk_scales_raw", [P, D], U8)
-        c_raw = new_tile("c_raw", [P, PACK, J], F32)
+        c_raw = [new_tile("c_raw%d" % half, [P, PACK, HALF], F32) for half in range(2)]
         x_raw = new_tile("x_raw", [P, PACK, M], F32)
         w_raw = span_tiles("w_raw", [P, PACK, SPAN], F32)
         mask = new_tile("mask", [P, PACK, J], F32)
@@ -57,7 +60,7 @@ def tile_mix_kvw_mask_kernel(tc, x, w, c, wk_words, wk_scales, msk, out_0, out_1
         x_bf = new_tile("x_bf", [P, M, PACK], BF16)
         w_bf = span_tiles("w_bf", [P, SPAN, PACK], BF16)
         k_bf = span_tiles("k_bf", [P, J, PACK], BF16)
-        q_bf = span_tiles("q_bf", [P, M, PACK], BF16)
+        q_bf = new_tile("q_bf", [P, D_SPANS * M, PACK], BF16)
         wk_dealt_words = new_tile("wk_dealt_words", [P, FP4_BYTES * D], U8)
         wk_dealt_scales = new_tile("wk_dealt_scales", [P, D], U8)
         c_codes = new_tile("c_codes", [P, J], U32)
@@ -66,18 +69,18 @@ def tile_mix_kvw_mask_kernel(tc, x, w, c, wk_words, wk_scales, msk, out_0, out_1
         x_scales = new_tile("x_scales", [P, M], U8)
         w_codes = span_tiles("w_codes", [P, SPAN], U32)
         w_scales = span_tiles("w_scales", [P, SPAN], U8)
-        q_codes = span_tiles("q_codes", [P, M], U32)
-        q_scales = span_tiles("q_scales", [P, M], U8)
-        k_codes = span_tiles("k_codes", [P, J], U32)
+        q_codes = new_tile("q_codes", [P, D_SPANS * M], U32)
+        q_scales = new_tile("q_scales", [P, D_SPANS * M], U8)
+        k_codes = new_tile("k_codes", [P, D_SPANS, J], U32)
         k_scales = new_tile("k_scales", [P, D_SPANS, J], U8)
         k_f32 = span_tiles("k_f32", [P, PACK, J], F32)
         scores = new_tile("scores", [P, PACK, J], F32)
 
         def deal_wk_words(a):
-            byte_cols = slice(FP4_BYTES * SPAN * a, FP4_BYTES * SPAN * (a + 1))
+            cols = slice(SPAN * a, SPAN * (a + 1))
             nc.vector.tensor_copy(
-                out=wk_dealt_words[:, byte_cols].rearrange("p (r n b) -> p r n b", r=PACK, b=FP4_BYTES),
-                in_=wk_words_raw[:, byte_cols].rearrange("p (n r b) -> p r n b", r=PACK, b=FP4_BYTES),
+                out=wk_dealt_words[:].bitcast(U16)[:, cols].rearrange("p (r n) -> p r n", r=PACK),
+                in_=wk_words_raw[:].bitcast(U16)[:, cols].rearrange("p (n r) -> p r n", r=PACK),
             )
 
         def deal_wk_scales(a):
@@ -93,11 +96,14 @@ def tile_mix_kvw_mask_kernel(tc, x, w, c, wk_words, wk_scales, msk, out_0, out_1
                 in_=raw[:, :, cols].rearrange("p t (g i) -> p g t i", i=PACK),
             )
 
-        def round_dealt(copy, staged, raw, half):
+        def round_c(copy, half, cols):
+            round_columns(copy, c_bf[:, halves[half], :], c_raw[half], cols)
+
+        def round_dealt(copy, staged, raw, half, ns):
             groups = slice(2 * half, 2 * half + 2)
             copy(
-                out=staged[:].rearrange("p (r n) t -> p n t r", r=PACK)[:, :, :, groups],
-                in_=raw[:].rearrange("p t (n r) -> p n t r", r=PACK)[:, :, :, groups],
+                out=staged[:].rearrange("p (r n) t -> p n t r", r=PACK)[:, ns, :, groups],
+                in_=raw[:].rearrange("p t (n r) -> p n t r", r=PACK)[:, ns, :, groups],
             )
 
         def quantize(codes, scales, staged, cols):
@@ -106,6 +112,9 @@ def tile_mix_kvw_mask_kernel(tc, x, w, c, wk_words, wk_scales, msk, out_0, out_1
                 scales=scales[:, cols],
                 in_=staged[:, cols, :].rearrange("p n t -> p (n t)"),
             )
+
+        def quantize_keys(a, cols):
+            quantize(k_codes[:, a, :], k_scales[:, a, :], k_bf[a], cols)
 
         def key_pass(out, a, r, js):
             col = SPAN * a + P * r
@@ -119,22 +128,14 @@ def tile_mix_kvw_mask_kernel(tc, x, w, c, wk_words, wk_scales, msk, out_0, out_1
                 stop=True,
             )
 
-        def keys_by_halves(a):
-            for half, js in enumerate(halves):
-                for pair in range(2):
-                    acc = bank(PACK * a + 2 * half + pair, "k_acc")
-                    for i in range(2):
-                        key_pass(acc[:, halves[i]], a, 2 * pair + i, js)
-                    nc.scalar.copy(
-                        out=k_f32[a][:, 2 * pair : 2 * pair + 2, js],
-                        in_=acc[:].rearrange("p (i j) -> p i j", i=2),
-                    )
-
-        def keys_whole(a):
-            for r in range(PACK):
-                acc = bank(PACK * a + r, "k_acc")
-                key_pass(acc[:], a, r, whole)
-                nc.scalar.copy(out=k_f32[a][:, r, :], in_=acc[:])
+        def key_bank(number, copy, a, half, pair):
+            acc = bank(number, "k_acc")
+            for i in range(2):
+                key_pass(acc[:, halves[i]], a, 2 * pair + i, halves[half])
+            copy(
+                out=k_f32[a][:, 2 * pair : 2 * pair + 2, halves[half]],
+                in_=acc[:].rearrange("p (i j) -> p i j", i=2),
+            )
 
         def store_keys(a):
             nc.sync.dma_start(
@@ -142,45 +143,63 @@ def tile_mix_kvw_mask_kernel(tc, x, w, c, wk_words, wk_scales, msk, out_0, out_1
                 in_=k_f32[a][:],
             )
 
-        def quantize_and_store_keys(a):
-            quantize(k_codes[a], k_scales[:, a, :], k_bf[a], whole)
+        def store_planes():
             nc.sync.dma_start(
-                out=out_2[a].rearrange("p j i -> p (j i)").bitcast(I32),
-                in_=k_codes[a][:].bitcast(I32),
+                out=out_2.rearrange("a p j i -> p a (j i)").bitcast(I32),
+                in_=k_codes[:].bitcast(I32),
+            )
+            for quad in range(QUADRANTS):
+                nc.sync.dma_start(
+                    out=out_3[:, 4 * quad : 4 * quad + 4, :].rearrange("a q j -> q a j").bitcast(I32),
+                    in_=k_scales[32 * quad : 32 * quad + 4, :, :].bitcast(I32),
+                )
+
+        def query_cols(s, a, spans):
+            first = P * (D_SPANS * s + a)
+            return slice(first, first + P * spans)
+
+        query_acc = {}
+
+        def query_passes(a, s, number):
+            acc = bank(number, "q_acc")
+            query_acc[a, s] = acc
+            ms = slice(P * s, P * (s + 1))
+            for r in range(PACK):
+                group = slice(P * r, P * (r + 1))
+                nc.tensor.matmul_mx(
+                    out=acc[:, group],
+                    lhsT=w_codes[a][:, group].bitcast(FP8X4),
+                    lhsT_scale=w_scales[a][:, group],
+                    rhs=x_codes[:, ms].bitcast(FP8X4),
+                    rhs_scale=x_scales[:, ms],
+                    start=True,
+                    stop=True,
+                )
+
+        def round_queries(copy, a, s):
+            copy(
+                out=q_bf[:, query_cols(s, a, 1), :],
+                in_=query_acc[a, s][:].rearrange("p (r n) -> p n r", r=PACK),
             )
 
-        def queries(a):
-            for s in range(PACK):
-                acc = bank(PACK * a + s, "q_acc")
-                ms = slice(P * s, P * (s + 1))
-                for r in range(PACK):
-                    group = slice(P * r, P * (r + 1))
-                    nc.tensor.matmul_mx(
-                        out=acc[:, group],
-                        lhsT=w_codes[a][:, group].bitcast(FP8X4),
-                        lhsT_scale=w_scales[a][:, group],
-                        rhs=x_codes[:, ms].bitcast(FP8X4),
-                        rhs_scale=x_scales[:, ms],
-                        start=True,
-                        stop=True,
-                    )
-                nc.scalar.copy(out=q_bf[a][:, ms, :], in_=acc[:].rearrange("p (r n) -> p n r", r=PACK))
+        def quantize_queries(s, a, spans):
+            quantize(q_codes, q_scales, q_bf, query_cols(s, a, spans))
 
-        def score_pass(s, a):
-            ms = slice(P * s, P * (s + 1))
+        score_acc = {}
+
+        def score_pass(s, a, number):
+            if a == 0:
+                score_acc[s] = bank(number, "s_acc")
+            cols = query_cols(s, a, 1)
             nc.tensor.matmul_mx(
                 out=score_acc[s][:],
-                lhsT=q_codes[a][:, ms].bitcast(FP8X4),
-                lhsT_scale=q_scales[a][:, ms],
-                rhs=k_codes[a][:].bitcast(FP8X4),
+                lhsT=q_codes[:, cols].bitcast(FP8X4),
+                lhsT_scale=q_scales[:, cols],
+                rhs=k_codes[:, a, :].bitcast(FP8X4),
                 rhs_scale=k_scales[:, a, :],
                 start=(a == 0),
                 stop=(a == D_SPANS - 1),
             )
-
-        def close_score_tile(s):
-            quantize(q_codes[1], q_scales[1], q_bf[1], slice(P * s, P * (s + 1)))
-            score_pass(s, 1)
 
         def finish_score_tile(s):
             nc.vector.scalar_tensor_tensor(
@@ -191,77 +210,90 @@ def tile_mix_kvw_mask_kernel(tc, x, w, c, wk_words, wk_scales, msk, out_0, out_1
                 op0=ALU.mult,
                 op1=ALU.add,
             )
-            nc.sync.dma_start(out=out_0.rearrange("(p s) j -> p s j", s=PACK)[:, s, :], in_=scores[:, s, :])
+
+        def store_scores(tiles):
+            nc.sync.dma_start(out=out_0.rearrange("(p s) j -> p s j", s=PACK)[:, tiles, :], in_=scores[:, tiles, :])
+
+        def load_rows(raw, source):
+            nc.sync.dma_start(out=raw[:], in_=source.rearrange("(p t) n -> p t n", t=PACK))
+
+        def load_wk_words():
+            nc.sync.dma_start(out=wk_words_raw[:].bitcast(I32), in_=wk_words[0].bitcast(I32))
+
+        def load_wk_scales():
+            for quad in range(QUADRANTS):
+                nc.sync.dma_start(
+                    out=wk_scales_raw[32 * quad : 32 * quad + 4, :].bitcast(I32),
+                    in_=wk_scales[0, 4 * quad : 4 * quad + 4, :].bitcast(I32),
+                )
+
+        vector, scalar = nc.vector.tensor_copy, nc.scalar.copy
+        every = slice(0, P)
 
         nc.vector.memset(wk_scales_raw[:].bitcast(I32), 0)
-        nc.sync.dma_start(out=wk_words_raw[:].bitcast(I32), in_=wk_words[0].bitcast(I32))
-        for quad in range(QUADRANTS):
-            nc.sync.dma_start(
-                out=wk_scales_raw[32 * quad : 32 * quad + 4, :].bitcast(I32),
-                in_=wk_scales[0, 4 * quad : 4 * quad + 4, :].bitcast(I32),
-            )
-        nc.sync.dma_start(out=c_raw[:], in_=c.rearrange("(p t) j -> p t j", t=PACK))
-        nc.sync.dma_start(out=x_raw[:], in_=x.rearrange("(p t) m -> p t m", t=PACK))
+        load_wk_words()
+        load_wk_scales()
+        for half in range(2):
+            load_rows(c_raw[half], c[:, halves[half]])
+        load_rows(x_raw, x)
         for a in range(D_SPANS):
-            nc.sync.dma_start(
-                out=w_raw[a][:],
-                in_=w[:, a * SPAN : (a + 1) * SPAN].rearrange("(p t) d -> p t d", t=PACK),
-            )
+            load_rows(w_raw[a], w[:, a * SPAN : (a + 1) * SPAN])
+        load_rows(mask, msk)
 
-        deal_wk_words(0)
-        deal_wk_scales(0)
-        deal_wk_words(1)
-        for cols in halves:
-            round_columns(nc.vector.tensor_copy, c_bf, c_raw, slice(cols.start, cols.start + C_VECTOR_COLS))
-            round_columns(nc.scalar.copy, c_bf, c_raw, slice(cols.start + C_VECTOR_COLS, cols.stop))
-        for cols in halves:
-            quantize(c_codes, c_scales, c_bf, cols)
-        deal_wk_scales(1)
+        for a in range(D_SPANS):
+            deal_wk_words(a)
+            deal_wk_scales(a)
+        for half in range(2):
+            round_c(vector, half, slice(0, C_VECTOR_COLS))
+            round_c(scalar, half, slice(C_VECTOR_COLS, HALF))
+            quantize(c_codes, c_scales, c_bf, halves[half])
 
-        keys_by_halves(0)
-        store_keys(0)
-        nc.sync.dma_start(out=mask[:], in_=msk.rearrange("(p s) j -> p s j", s=PACK))
-        keys_whole(1)
-        store_keys(1)
+        for a in range(D_SPANS):
+            for half in range(2):
+                for pair in range(2):
+                    key_bank(2 * half + pair, scalar, a, half, pair)
+            store_keys(a)
+        for half in range(2):
+            round_dealt(vector, x_bf, x_raw, half, every)
+        round_columns(vector, k_bf[0], k_f32[0], slice(0, KEYS_FIRST_END))
+        quantize(x_codes, x_scales, x_bf, whole)
 
         for half in range(2):
-            round_dealt(nc.vector.tensor_copy, x_bf, x_raw, half)
-        for cols in halves:
-            quantize(x_codes, x_scales, x_bf, cols)
-        round_columns(nc.vector.tensor_copy, k_bf[0], k_f32[0], slice(0, KEYS_EARLY_END))
-        for half in range(2):
-            round_dealt(nc.vector.tensor_copy, w_bf[0], w_raw[0], half)
+            round_dealt(vector, w_bf[0], w_raw[0], half, every)
         for cols in halves:
             quantize(w_codes[0], w_scales[0], w_bf[0], cols)
-
-        round_columns(nc.scalar.copy, k_bf[0], k_f32[0], slice(KEYS_SCALAR_START, J))
-        round_dealt(nc.scalar.copy, w_bf[1], w_raw[1], 1)
-        queries(0)
-        round_columns(nc.vector.tensor_copy, k_bf[0], k_f32[0], slice(KEYS_EARLY_END, KEYS_SCALAR_START))
-        round_dealt(nc.vector.tensor_copy, w_bf[1], w_raw[1], 0)
-        quantize_and_store_keys(0)
-        quantize(w_codes[1], w_scales[1], w_bf[1], whole)
-        queries(1)
-        round_columns(nc.vector.tensor_copy, k_bf[1], k_f32[1], whole)
-
-        score_acc = [bank(s, "s_acc") for s in range(PACK)]
-        quantize(q_codes[0], q_scales[0], q_bf[0], halves[0])
-        score_pass(0, 0)
-        score_pass(1, 0)
-        quantize_and_store_keys(1)
-        for quad in range(QUADRANTS):
-            nc.sync.dma_start(
-                out=out_3[:, 4 * quad : 4 * quad + 4, :].rearrange("a q j -> q a j").bitcast(I32),
-                in_=k_scales[32 * quad : 32 * quad + 4, :, :].bitcast(I32),
-            )
-
-        close_score_tile(0)
-        quantize(q_codes[0], q_scales[0], q_bf[0], halves[1])
-        score_pass(2, 0)
-        close_score_tile(1)
-        score_pass(3, 0)
-        finish_score_tile(0)
+        round_columns(vector, k_bf[0], k_f32[0], slice(KEYS_FIRST_END, KEYS_SECOND_END))
+        round_columns(scalar, k_bf[1], k_f32[1], slice(0, KEYS_SCALAR_COLS))
+        for s in range(PACK):
+            query_passes(0, s, 4 + s)
+        round_dealt(vector, w_bf[1], w_raw[1], 0, every)
+        round_dealt(scalar, w_bf[1], w_raw[1], 1, slice(W1_SPLIT, P))
+        round_dealt(vector, w_bf[1], w_raw[1], 1, slice(0, W1_SPLIT))
+        for s in range(3):
+            round_queries(scalar, 0, s)
+        for cols in halves:
+            quantize(w_codes[1], w_scales[1], w_bf[1], cols)
+        for s in range(PACK):
+            query_passes(1, s, s)
+        for s in range(3):
+            round_queries(scalar, 1, s)
+        for a in range(D_SPANS):
+            round_queries(scalar, a, 3)
+        round_columns(vector, k_bf[0], k_f32[0], slice(KEYS_SECOND_END, J))
+        round_columns(vector, k_bf[1], k_f32[1], slice(KEYS_SCALAR_COLS, J))
+        quantize_keys(0, whole)
+        quantize_queries(0, 0, 2)
+        score_pass(0, 0, 4)
+        quantize_keys(1, whole)
+        store_planes()
+        score_pass(0, 1, 4)
+        for s in range(1, PACK):
+            quantize_queries(s, 0, 2)
+            for a in range(D_SPANS):
+                score_pass(s, a, 4 + s)
+            if s > 1:
+                finish_score_tile(s - 2)
+                store_scores(slice(s - 2, s - 1))
         for s in range(2, PACK):
-            close_score_tile(s)
-            finish_score_tile(s - 1)
-        finish_score_tile(PACK - 1)
+            finish_score_tile(s)
+            store_scores(slice(s, s + 1))

@@ -20,15 +20,16 @@ PACK = 4
 SPAN = P * PACK
 HALF = SPAN // 2
 D_SPANS = D // SPAN
-QUADRANTS = 4
+BLOCK = 32
+QUADRANT = 32
+SCALE_ROWS = 4
 FP4_BYTES = 2
 SCORE_SCALE = 0.03125
 
-C_VECTOR_COLS = 160
 W1_SPLIT = 40
 KEYS_FIRST_END = 128
 KEYS_SECOND_END = 256
-KEYS_SCALAR_COLS = 224
+KEYS_SCALAR_COLS = 96
 
 
 def tile_mix_kvw_mask_kernel(tc, x, w, c, wk_words, wk_scales, msk, out_0, out_1, out_2, out_3):
@@ -52,7 +53,7 @@ def tile_mix_kvw_mask_kernel(tc, x, w, c, wk_words, wk_scales, msk, out_0, out_1
 
         wk_words_raw = new_tile("wk_words_raw", [P, FP4_BYTES * D], U8)
         wk_scales_raw = new_tile("wk_scales_raw", [P, D], U8)
-        c_raw = [new_tile("c_raw%d" % half, [P, PACK, HALF], F32) for half in range(2)]
+        c_raw = new_tile("c_raw", [P, PACK, J], F32)
         x_raw = new_tile("x_raw", [P, PACK, M], F32)
         w_raw = span_tiles("w_raw", [P, PACK, SPAN], F32)
         mask = new_tile("mask", [P, PACK, J], F32)
@@ -95,9 +96,6 @@ def tile_mix_kvw_mask_kernel(tc, x, w, c, wk_words, wk_scales, msk, out_0, out_1
                 out=staged[:, cols, :].rearrange("p (g i) t -> p g t i", i=PACK),
                 in_=raw[:, :, cols].rearrange("p t (g i) -> p g t i", i=PACK),
             )
-
-        def round_c(copy, half, cols):
-            round_columns(copy, c_bf[:, halves[half], :], c_raw[half], cols)
 
         def round_dealt(copy, staged, raw, half, ns):
             groups = slice(2 * half, 2 * half + 2)
@@ -148,10 +146,10 @@ def tile_mix_kvw_mask_kernel(tc, x, w, c, wk_words, wk_scales, msk, out_0, out_1
                 out=out_2.rearrange("a p j i -> p a (j i)").bitcast(I32),
                 in_=k_codes[:].bitcast(I32),
             )
-            for quad in range(QUADRANTS):
+            for row in range(SCALE_ROWS):
                 nc.sync.dma_start(
-                    out=out_3[:, 4 * quad : 4 * quad + 4, :].rearrange("a q j -> q a j").bitcast(I32),
-                    in_=k_scales[32 * quad : 32 * quad + 4, :, :].bitcast(I32),
+                    out=out_3[:, row : P * PACK // BLOCK : SCALE_ROWS, :].rearrange("a q j -> q a j").bitcast(I32),
+                    in_=k_scales[row:P:QUADRANT, :, :].bitcast(I32),
                 )
 
         def query_cols(s, a, spans):
@@ -221,32 +219,32 @@ def tile_mix_kvw_mask_kernel(tc, x, w, c, wk_words, wk_scales, msk, out_0, out_1
             nc.sync.dma_start(out=wk_words_raw[:].bitcast(I32), in_=wk_words[0].bitcast(I32))
 
         def load_wk_scales():
-            for quad in range(QUADRANTS):
+            for row in range(SCALE_ROWS):
                 nc.sync.dma_start(
-                    out=wk_scales_raw[32 * quad : 32 * quad + 4, :].bitcast(I32),
-                    in_=wk_scales[0, 4 * quad : 4 * quad + 4, :].bitcast(I32),
+                    out=wk_scales_raw[row:P:QUADRANT, :].bitcast(I32),
+                    in_=wk_scales[0, row : P * PACK // BLOCK : SCALE_ROWS, :].bitcast(I32),
                 )
 
         vector, scalar = nc.vector.tensor_copy, nc.scalar.copy
         every = slice(0, P)
 
         nc.vector.memset(wk_scales_raw[:].bitcast(I32), 0)
-        load_wk_words()
+        load_rows(c_raw, c)
         load_wk_scales()
-        for half in range(2):
-            load_rows(c_raw[half], c[:, halves[half]])
+        load_wk_words()
         load_rows(x_raw, x)
         for a in range(D_SPANS):
             load_rows(w_raw[a], w[:, a * SPAN : (a + 1) * SPAN])
         load_rows(mask, msk)
 
-        for a in range(D_SPANS):
-            deal_wk_words(a)
-            deal_wk_scales(a)
-        for half in range(2):
-            round_c(vector, half, slice(0, C_VECTOR_COLS))
-            round_c(scalar, half, slice(C_VECTOR_COLS, HALF))
-            quantize(c_codes, c_scales, c_bf, halves[half])
+        round_columns(vector, c_bf, c_raw, halves[0])
+        round_columns(scalar, c_bf, c_raw, halves[1])
+        deal_wk_scales(0)
+        quantize(c_codes, c_scales, c_bf, halves[0])
+        deal_wk_words(0)
+        quantize(c_codes, c_scales, c_bf, halves[1])
+        deal_wk_words(1)
+        deal_wk_scales(1)
 
         for a in range(D_SPANS):
             for half in range(2):

@@ -26,10 +26,13 @@ SCALE_ROWS = 4
 FP4_BYTES = 2
 SCORE_SCALE = 0.03125
 
+LAST = PACK - 1
+C_VECTOR_COLS = 160
 W1_SPLIT = 40
 KEYS_FIRST_END = 128
 KEYS_SECOND_END = 256
-KEYS_SCALAR_COLS = 96
+KEYS_EARLY_COLS = 192
+KEYS_SCALAR_COLS = 256
 
 
 def tile_mix_kvw_mask_kernel(tc, x, w, c, wk_words, wk_scales, msk, out_0, out_1, out_2, out_3):
@@ -77,19 +80,18 @@ def tile_mix_kvw_mask_kernel(tc, x, w, c, wk_words, wk_scales, msk, out_0, out_1
         k_f32 = span_tiles("k_f32", [P, PACK, J], F32)
         scores = new_tile("scores", [P, PACK, J], F32)
 
-        def deal_wk_words(a):
+        def deal(dealt, raw, a, groups):
             cols = slice(SPAN * a, SPAN * (a + 1))
             nc.vector.tensor_copy(
-                out=wk_dealt_words[:].bitcast(U16)[:, cols].rearrange("p (r n) -> p r n", r=PACK),
-                in_=wk_words_raw[:].bitcast(U16)[:, cols].rearrange("p (n r) -> p r n", r=PACK),
+                out=dealt[:, cols].rearrange("p (r n) -> p r n", r=PACK)[:, groups, :],
+                in_=raw[:, cols].rearrange("p (n r) -> p r n", r=PACK)[:, groups, :],
             )
 
-        def deal_wk_scales(a):
-            cols = slice(SPAN * a, SPAN * (a + 1))
-            nc.vector.tensor_copy(
-                out=wk_dealt_scales[:, cols].rearrange("p (r n) -> p r n", r=PACK),
-                in_=wk_scales_raw[:, cols].rearrange("p (n r) -> p r n", r=PACK),
-            )
+        def deal_wk_words(a, groups):
+            deal(wk_dealt_words[:].bitcast(U16), wk_words_raw[:].bitcast(U16), a, groups)
+
+        def deal_wk_scales(a, groups):
+            deal(wk_dealt_scales[:], wk_scales_raw[:], a, groups)
 
         def round_columns(copy, staged, raw, cols):
             copy(
@@ -227,6 +229,8 @@ def tile_mix_kvw_mask_kernel(tc, x, w, c, wk_words, wk_scales, msk, out_0, out_1
 
         vector, scalar = nc.vector.tensor_copy, nc.scalar.copy
         every = slice(0, P)
+        pairs = [slice(0, 2), slice(2, PACK)]
+        all_groups = slice(0, PACK)
 
         nc.vector.memset(wk_scales_raw[:].bitcast(I32), 0)
         load_rows(c_raw, c)
@@ -237,14 +241,17 @@ def tile_mix_kvw_mask_kernel(tc, x, w, c, wk_words, wk_scales, msk, out_0, out_1
             load_rows(w_raw[a], w[:, a * SPAN : (a + 1) * SPAN])
         load_rows(mask, msk)
 
-        round_columns(vector, c_bf, c_raw, halves[0])
+        round_columns(vector, c_bf, c_raw, slice(0, C_VECTOR_COLS))
+        round_columns(scalar, c_bf, c_raw, slice(C_VECTOR_COLS, HALF))
         round_columns(scalar, c_bf, c_raw, halves[1])
-        deal_wk_scales(0)
+        deal_wk_scales(0, pairs[0])
         quantize(c_codes, c_scales, c_bf, halves[0])
-        deal_wk_words(0)
+        deal_wk_words(0, pairs[0])
+        deal_wk_words(0, pairs[1])
+        deal_wk_scales(0, pairs[1])
+        deal_wk_words(1, all_groups)
         quantize(c_codes, c_scales, c_bf, halves[1])
-        deal_wk_words(1)
-        deal_wk_scales(1)
+        deal_wk_scales(1, all_groups)
 
         for a in range(D_SPANS):
             for half in range(2):
@@ -261,29 +268,31 @@ def tile_mix_kvw_mask_kernel(tc, x, w, c, wk_words, wk_scales, msk, out_0, out_1
         for cols in halves:
             quantize(w_codes[0], w_scales[0], w_bf[0], cols)
         round_columns(vector, k_bf[0], k_f32[0], slice(KEYS_FIRST_END, KEYS_SECOND_END))
-        round_columns(scalar, k_bf[1], k_f32[1], slice(0, KEYS_SCALAR_COLS))
+        round_columns(scalar, k_bf[1], k_f32[1], slice(0, KEYS_EARLY_COLS))
         for s in range(PACK):
             query_passes(0, s, 4 + s)
         round_dealt(vector, w_bf[1], w_raw[1], 0, every)
         round_dealt(scalar, w_bf[1], w_raw[1], 1, slice(W1_SPLIT, P))
         round_dealt(vector, w_bf[1], w_raw[1], 1, slice(0, W1_SPLIT))
-        for s in range(3):
+        round_columns(scalar, k_bf[1], k_f32[1], slice(KEYS_EARLY_COLS, KEYS_SCALAR_COLS))
+        for s in range(LAST):
             round_queries(scalar, 0, s)
         for cols in halves:
             quantize(w_codes[1], w_scales[1], w_bf[1], cols)
         for s in range(PACK):
             query_passes(1, s, s)
-        for s in range(3):
+        for s in range(LAST):
             round_queries(scalar, 1, s)
         for a in range(D_SPANS):
-            round_queries(scalar, a, 3)
+            round_queries(scalar, a, LAST)
         round_columns(vector, k_bf[0], k_f32[0], slice(KEYS_SECOND_END, J))
         round_columns(vector, k_bf[1], k_f32[1], slice(KEYS_SCALAR_COLS, J))
         quantize_keys(0, whole)
-        quantize_queries(0, 0, 2)
+        quantize_queries(0, 0, 1)
         score_pass(0, 0, 4)
         quantize_keys(1, whole)
         store_planes()
+        quantize_queries(0, 1, 1)
         score_pass(0, 1, 4)
         for s in range(1, PACK):
             quantize_queries(s, 0, 2)

@@ -31,8 +31,8 @@ C_VECTOR_COLS = 160
 W1_SPLIT = 40
 KEYS_FIRST_END = 128
 KEYS_SECOND_END = 256
-KEYS_EARLY_COLS = 192
-KEYS_SCALAR_COLS = 256
+KEYS_EARLY_COLS = 160
+KEYS_SCALAR_COLS = 224
 
 
 def tile_mix_kvw_mask_kernel(tc, x, w, c, wk_words, wk_scales, msk, out_0, out_1, out_2, out_3):
@@ -77,7 +77,8 @@ def tile_mix_kvw_mask_kernel(tc, x, w, c, wk_words, wk_scales, msk, out_0, out_1
         q_scales = new_tile("q_scales", [P, D_SPANS * M], U8)
         k_codes = new_tile("k_codes", [P, D_SPANS, J], U32)
         k_scales = new_tile("k_scales", [P, D_SPANS, J], U8)
-        k_f32 = span_tiles("k_f32", [P, PACK, J], F32)
+        k_all = new_tile("k_f32", [P, D_SPANS, PACK, J], F32)
+        k_f32 = [k_all[:, a] for a in range(D_SPANS)]
         scores = new_tile("scores", [P, PACK, J], F32)
 
         def deal(dealt, raw, a, groups):
@@ -137,11 +138,8 @@ def tile_mix_kvw_mask_kernel(tc, x, w, c, wk_words, wk_scales, msk, out_0, out_1
                 in_=acc[:].rearrange("p (i j) -> p i j", i=2),
             )
 
-        def store_keys(a):
-            nc.sync.dma_start(
-                out=out_1[a * SPAN : (a + 1) * SPAN, :].rearrange("(p r) j -> p r j", r=PACK),
-                in_=k_f32[a][:],
-            )
+        def store_keys():
+            nc.sync.dma_start(out=out_1.rearrange("(a p r) j -> p a r j", a=D_SPANS, r=PACK), in_=k_all[:])
 
         def store_planes():
             nc.sync.dma_start(
@@ -257,7 +255,7 @@ def tile_mix_kvw_mask_kernel(tc, x, w, c, wk_words, wk_scales, msk, out_0, out_1
             for half in range(2):
                 for pair in range(2):
                     key_bank(2 * half + pair, scalar, a, half, pair)
-            store_keys(a)
+        store_keys()
         for half in range(2):
             round_dealt(vector, x_bf, x_raw, half, every)
         round_columns(vector, k_bf[0], k_f32[0], slice(0, KEYS_FIRST_END))

@@ -28,11 +28,11 @@ SCORE_SCALE = 0.03125
 
 LAST = PACK - 1
 C_VECTOR_COLS = 160
-W1_SPLIT = 40
+W1_SPLIT = 56
 KEYS_FIRST_END = 128
 KEYS_SECOND_END = 256
 KEYS_EARLY_COLS = 160
-KEYS_SCALAR_COLS = 224
+KEYS_SCALAR_COLS = 256
 
 
 def tile_mix_kvw_mask_kernel(tc, x, w, c, wk_words, wk_scales, msk, out_0, out_1, out_2, out_3):
@@ -209,6 +209,23 @@ def tile_mix_kvw_mask_kernel(tc, x, w, c, wk_words, wk_scales, msk, out_0, out_1
                 op1=ALU.add,
             )
 
+        def open_tile(s):
+            quantize_queries(s, 0, 1)
+            score_pass(s, 0, 4 + s)
+
+        def close_tile(s):
+            quantize_queries(s, 1, 1)
+            score_pass(s, 1, 4 + s)
+
+        def both(s):
+            quantize_queries(s, 0, 2)
+            for a in range(D_SPANS):
+                score_pass(s, a, 4 + s)
+
+        def fin(s):
+            finish_score_tile(s)
+            store_scores(slice(s, s + 1))
+
         def store_scores(tiles):
             nc.sync.dma_start(out=out_0.rearrange("(p s) j -> p s j", s=PACK)[:, tiles, :], in_=scores[:, tiles, :])
 
@@ -242,11 +259,10 @@ def tile_mix_kvw_mask_kernel(tc, x, w, c, wk_words, wk_scales, msk, out_0, out_1
         round_columns(vector, c_bf, c_raw, slice(0, C_VECTOR_COLS))
         round_columns(scalar, c_bf, c_raw, slice(C_VECTOR_COLS, HALF))
         round_columns(scalar, c_bf, c_raw, halves[1])
-        deal_wk_scales(0, pairs[0])
+        deal_wk_scales(0, all_groups)
         quantize(c_codes, c_scales, c_bf, halves[0])
         deal_wk_words(0, pairs[0])
         deal_wk_words(0, pairs[1])
-        deal_wk_scales(0, pairs[1])
         deal_wk_words(1, all_groups)
         quantize(c_codes, c_scales, c_bf, halves[1])
         deal_wk_scales(1, all_groups)
@@ -256,8 +272,10 @@ def tile_mix_kvw_mask_kernel(tc, x, w, c, wk_words, wk_scales, msk, out_0, out_1
                 for pair in range(2):
                     key_bank(2 * half + pair, scalar, a, half, pair)
         store_keys()
-        for half in range(2):
-            round_dealt(vector, x_bf, x_raw, half, every)
+        vector(
+            out=x_bf[:].rearrange("p (r n) t -> p n t r", r=PACK),
+            in_=x_raw[:].rearrange("p t (n r) -> p n t r", r=PACK),
+        )
         round_columns(vector, k_bf[0], k_f32[0], slice(0, KEYS_FIRST_END))
         quantize(x_codes, x_scales, x_bf, whole)
 
@@ -273,32 +291,30 @@ def tile_mix_kvw_mask_kernel(tc, x, w, c, wk_words, wk_scales, msk, out_0, out_1
         round_dealt(scalar, w_bf[1], w_raw[1], 1, slice(W1_SPLIT, P))
         round_dealt(vector, w_bf[1], w_raw[1], 1, slice(0, W1_SPLIT))
         round_columns(scalar, k_bf[1], k_f32[1], slice(KEYS_EARLY_COLS, KEYS_SCALAR_COLS))
-        for s in range(LAST):
-            round_queries(scalar, 0, s)
+        round_queries(scalar, 0, 0)
+        round_queries(scalar, 0, 1)
+        round_queries(scalar, 0, 2)
         for cols in halves:
             quantize(w_codes[1], w_scales[1], w_bf[1], cols)
         for s in range(PACK):
             query_passes(1, s, s)
-        for s in range(LAST):
-            round_queries(scalar, 1, s)
-        for a in range(D_SPANS):
-            round_queries(scalar, a, LAST)
+        round_queries(scalar, 1, 0)
+        round_queries(scalar, 1, 1)
+        round_queries(scalar, 1, 2)
+        round_queries(scalar, 0, 3)
+        round_queries(scalar, 1, 3)
         round_columns(vector, k_bf[0], k_f32[0], slice(KEYS_SECOND_END, J))
         round_columns(vector, k_bf[1], k_f32[1], slice(KEYS_SCALAR_COLS, J))
         quantize_keys(0, whole)
-        quantize_queries(0, 0, 1)
-        score_pass(0, 0, 4)
+        open_tile(0)
         quantize_keys(1, whole)
         store_planes()
-        quantize_queries(0, 1, 1)
-        score_pass(0, 1, 4)
-        for s in range(1, PACK):
-            quantize_queries(s, 0, 2)
-            for a in range(D_SPANS):
-                score_pass(s, a, 4 + s)
-            if s > 1:
-                finish_score_tile(s - 2)
-                store_scores(slice(s - 2, s - 1))
-        for s in range(2, PACK):
-            finish_score_tile(s)
-            store_scores(slice(s, s + 1))
+        close_tile(0)
+        both(1)
+        both(2)
+        fin(0)
+        open_tile(3)
+        close_tile(3)
+        fin(1)
+        fin(2)
+        fin(3)

@@ -25,14 +25,7 @@ QUADRANT = 32
 SCALE_ROWS = 4
 FP4_BYTES = 2
 SCORE_SCALE = 0.03125
-
-LAST = PACK - 1
-C_VECTOR_COLS = 160
-W1_SPLIT = 56
-KEYS_FIRST_END = 128
-KEYS_SECOND_END = 256
-KEYS_EARLY_COLS = 160
-KEYS_SCALAR_COLS = 256
+KEY_SCALE_ROW = 4
 
 
 def tile_mix_kvw_mask_kernel(tc, x, w, c, wk_words, wk_scales, msk, out_0, out_1, out_2, out_3):
@@ -58,7 +51,8 @@ def tile_mix_kvw_mask_kernel(tc, x, w, c, wk_words, wk_scales, msk, out_0, out_1
         wk_scales_raw = new_tile("wk_scales_raw", [P, D], U8)
         c_raw = new_tile("c_raw", [P, PACK, J], F32)
         x_raw = new_tile("x_raw", [P, PACK, M], F32)
-        w_raw = span_tiles("w_raw", [P, PACK, SPAN], F32)
+        w_tiles = span_tiles("w_raw", [P, PACK, SPAN], F32)
+        w_raw = [tile[:] for tile in w_tiles]
         mask = new_tile("mask", [P, PACK, J], F32)
         c_bf = new_tile("c_bf", [P, J, PACK], BF16)
         x_bf = new_tile("x_bf", [P, M, PACK], BF16)
@@ -100,12 +94,20 @@ def tile_mix_kvw_mask_kernel(tc, x, w, c, wk_words, wk_scales, msk, out_0, out_1
                 in_=raw[:, :, cols].rearrange("p t (g i) -> p g t i", i=PACK),
             )
 
-        def round_dealt(copy, staged, raw, half, ns):
-            groups = slice(2 * half, 2 * half + 2)
+        def round_dealt(copy, staged, raw, groups, ns):
             copy(
-                out=staged[:].rearrange("p (r n) t -> p n t r", r=PACK)[:, ns, :, groups],
-                in_=raw[:].rearrange("p t (n r) -> p n t r", r=PACK)[:, ns, :, groups],
+                out=staged.rearrange("p (r n) t -> p n t r", r=PACK)[:, ns, :, groups],
+                in_=raw.rearrange("p t (n r) -> p n t r", r=PACK)[:, ns, :, groups],
             )
+
+        def round_w(copy, a, groups, ns):
+            round_dealt(copy, w_bf[a][:], w_raw[a], groups, ns)
+
+        def round_keys(copy, a, cols):
+            round_columns(copy, k_bf[a], k_f32[a], cols)
+
+        def round_x(copy, groups, ns):
+            round_dealt(copy, x_bf[:], x_raw[:], groups, ns)
 
         def quantize(codes, scales, staged, cols):
             nc.vector.quantize_mx(
@@ -115,7 +117,16 @@ def tile_mix_kvw_mask_kernel(tc, x, w, c, wk_words, wk_scales, msk, out_0, out_1
             )
 
         def quantize_keys(a, cols):
-            quantize(k_codes[:, a, :], k_scales[:, a, :], k_bf[a], cols)
+            quantize(k_codes[:, a, :], k_scales[KEY_SCALE_ROW:P, a, :], k_bf[a], cols)
+
+        def quantize_c(cols):
+            quantize(c_codes, c_scales, c_bf, cols)
+
+        def quantize_x(cols):
+            quantize(x_codes, x_scales, x_bf, cols)
+
+        def quantize_w(a, cols):
+            quantize(w_codes[a], w_scales[a], w_bf[a], cols)
 
         def key_pass(out, a, r, js):
             col = SPAN * a + P * r
@@ -129,27 +140,63 @@ def tile_mix_kvw_mask_kernel(tc, x, w, c, wk_words, wk_scales, msk, out_0, out_1
                 stop=True,
             )
 
-        def key_bank(number, copy, a, half, pair):
+        key_acc = {}
+
+        def key_passes(number, a, half, pair):
             acc = bank(number, "k_acc")
+            key_acc[a, half, pair] = acc
             for i in range(2):
                 key_pass(acc[:, halves[i]], a, 2 * pair + i, halves[half])
+
+        def key_columns(number, copy, a, js):
+            acc = bank(number, "k_acc")
+            for r in range(PACK):
+                key_pass(acc[:, P * r : P * (r + 1)], a, r, js)
+            copy(out=k_f32[a][:, :, js], in_=acc[:].rearrange("p (r j) -> p r j", r=PACK))
+
+        def key_group(number, copy, a, r):
+            acc = bank(number, "k_acc")
+            key_pass(acc[:], a, r, whole)
+            copy(out=k_f32[a][:, r, :], in_=acc[:])
+
+        def warm_up(passes):
+            zeros = new_tile("zeros", [P, SPAN, PACK], BF16)
+            zero_codes = new_tile("zero_codes", [P, SPAN], U32)
+            zero_scales = new_tile("zero_scales", [P, SPAN], U8)
+            nc.vector.memset(zeros[:].rearrange("p n t -> p (n t)").bitcast(I32), 0)
+            quantize(zero_codes, zero_scales, zeros, whole)
+            acc = bank(7, "warm_acc")
+            for unused in range(passes):
+                nc.tensor.matmul_mx(
+                    out=acc[:],
+                    lhsT=zero_codes[:, 0:P].bitcast(FP8X4),
+                    lhsT_scale=zero_scales[:, 0:P],
+                    rhs=zero_codes[:].bitcast(FP8X4),
+                    rhs_scale=zero_scales[:],
+                    start=True,
+                    stop=True,
+                )
+
+        def empty_keys(copy, a, half, pair):
             copy(
                 out=k_f32[a][:, 2 * pair : 2 * pair + 2, halves[half]],
-                in_=acc[:].rearrange("p (i j) -> p i j", i=2),
+                in_=key_acc[a, half, pair][:].rearrange("p (i j) -> p i j", i=2),
             )
 
         def store_keys():
             nc.sync.dma_start(out=out_1.rearrange("(a p r) j -> p a r j", a=D_SPANS, r=PACK), in_=k_all[:])
 
-        def store_planes():
+        def store_key_words():
             nc.sync.dma_start(
                 out=out_2.rearrange("a p j i -> p a (j i)").bitcast(I32),
                 in_=k_codes[:].bitcast(I32),
             )
+
+        def store_key_scales():
             for row in range(SCALE_ROWS):
                 nc.sync.dma_start(
                     out=out_3[:, row : P * PACK // BLOCK : SCALE_ROWS, :].rearrange("a q j -> q a j").bitcast(I32),
-                    in_=k_scales[row:P:QUADRANT, :, :].bitcast(I32),
+                    in_=k_scales[KEY_SCALE_ROW + row : P : QUADRANT, :, :].bitcast(I32),
                 )
 
         def query_cols(s, a, spans):
@@ -194,40 +241,39 @@ def tile_mix_kvw_mask_kernel(tc, x, w, c, wk_words, wk_scales, msk, out_0, out_1
                 lhsT=q_codes[:, cols].bitcast(FP8X4),
                 lhsT_scale=q_scales[:, cols],
                 rhs=k_codes[:, a, :].bitcast(FP8X4),
-                rhs_scale=k_scales[:, a, :],
+                rhs_scale=k_scales[KEY_SCALE_ROW:P, a, :],
                 start=(a == 0),
                 stop=(a == D_SPANS - 1),
             )
 
-        def finish_score_tile(s):
+        def finish(s, js):
             nc.vector.scalar_tensor_tensor(
-                out=scores[:, s, :],
-                in0=score_acc[s][:],
+                out=scores[:, s, js],
+                in0=score_acc[s][:, js],
                 scalar=SCORE_SCALE,
-                in1=mask[:, s, :],
+                in1=mask[:, s, js],
                 op0=ALU.mult,
                 op1=ALU.add,
             )
 
-        def open_tile(s):
+        def open_tile(s, number):
             quantize_queries(s, 0, 1)
-            score_pass(s, 0, 4 + s)
+            score_pass(s, 0, number)
 
-        def close_tile(s):
+        def close_tile(s, number):
             quantize_queries(s, 1, 1)
-            score_pass(s, 1, 4 + s)
+            score_pass(s, 1, number)
 
-        def both(s):
+        def both_spans(s, number):
             quantize_queries(s, 0, 2)
             for a in range(D_SPANS):
-                score_pass(s, a, 4 + s)
+                score_pass(s, a, number)
 
-        def fin(s):
-            finish_score_tile(s)
-            store_scores(slice(s, s + 1))
+        def store_scores(tiles, js):
+            nc.sync.dma_start(out=out_0.rearrange("(p s) j -> p s j", s=PACK)[:, tiles, js], in_=scores[:, tiles, js])
 
-        def store_scores(tiles):
-            nc.sync.dma_start(out=out_0.rearrange("(p s) j -> p s j", s=PACK)[:, tiles, :], in_=scores[:, tiles, :])
+        def load_mask():
+            nc.sync.dma_start(out=mask[:], in_=msk.rearrange("(p s) j -> p s j", s=PACK))
 
         def load_rows(raw, source):
             nc.sync.dma_start(out=raw[:], in_=source.rearrange("(p t) n -> p t n", t=PACK))
@@ -253,68 +299,72 @@ def tile_mix_kvw_mask_kernel(tc, x, w, c, wk_words, wk_scales, msk, out_0, out_1
         load_wk_words()
         load_rows(x_raw, x)
         for a in range(D_SPANS):
-            load_rows(w_raw[a], w[:, a * SPAN : (a + 1) * SPAN])
-        load_rows(mask, msk)
+            load_rows(w_tiles[a], w[:, a * SPAN : (a + 1) * SPAN])
+        load_mask()
 
-        round_columns(vector, c_bf, c_raw, slice(0, C_VECTOR_COLS))
-        round_columns(scalar, c_bf, c_raw, slice(C_VECTOR_COLS, HALF))
+
+        round_columns(vector, c_bf, c_raw, slice(0, 160))
+        round_columns(scalar, c_bf, c_raw, slice(160, HALF))
         round_columns(scalar, c_bf, c_raw, halves[1])
         deal_wk_scales(0, all_groups)
-        quantize(c_codes, c_scales, c_bf, halves[0])
+        quantize_c(halves[0])
         deal_wk_words(0, pairs[0])
         deal_wk_words(0, pairs[1])
         deal_wk_words(1, all_groups)
-        quantize(c_codes, c_scales, c_bf, halves[1])
+        quantize_c(halves[1])
         deal_wk_scales(1, all_groups)
-
-        for a in range(D_SPANS):
-            for half in range(2):
-                for pair in range(2):
-                    key_bank(2 * half + pair, scalar, a, half, pair)
-        store_keys()
-        vector(
-            out=x_bf[:].rearrange("p (r n) t -> p n t r", r=PACK),
-            in_=x_raw[:].rearrange("p t (n r) -> p n t r", r=PACK),
-        )
-        round_columns(vector, k_bf[0], k_f32[0], slice(0, KEYS_FIRST_END))
-        quantize(x_codes, x_scales, x_bf, whole)
-
         for half in range(2):
-            round_dealt(vector, w_bf[0], w_raw[0], half, every)
-        for cols in halves:
-            quantize(w_codes[0], w_scales[0], w_bf[0], cols)
-        round_columns(vector, k_bf[0], k_f32[0], slice(KEYS_FIRST_END, KEYS_SECOND_END))
-        round_columns(scalar, k_bf[1], k_f32[1], slice(0, KEYS_EARLY_COLS))
-        for s in range(PACK):
+            for pair in range(2):
+                key_passes(2 * half + pair, 0, half, pair)
+                empty_keys(vector if (half, pair) == (2, 2) else scalar, 0, half, pair)
+        for r in range(PACK):
+            key_group((PACK + r) % 4, scalar, 1, r)
+        store_keys()
+        round_x(vector, all_groups, every)
+        round_keys(vector, 0, slice(0, 128))
+        quantize_x(whole)
+        round_w(vector, 0, pairs[0], every)
+        round_w(vector, 0, pairs[1], every)
+        quantize_w(0, halves[0])
+        quantize_w(0, halves[1])
+        round_keys(vector, 0, slice(128, 256))
+        round_keys(scalar, 0, slice(256, 416))
+
+        for s in range(3):
             query_passes(0, s, 4 + s)
-        round_dealt(vector, w_bf[1], w_raw[1], 0, every)
-        round_dealt(scalar, w_bf[1], w_raw[1], 1, slice(W1_SPLIT, P))
-        round_dealt(vector, w_bf[1], w_raw[1], 1, slice(0, W1_SPLIT))
-        round_columns(scalar, k_bf[1], k_f32[1], slice(KEYS_EARLY_COLS, KEYS_SCALAR_COLS))
-        round_queries(scalar, 0, 0)
-        round_queries(scalar, 0, 1)
-        round_queries(scalar, 0, 2)
-        for cols in halves:
-            quantize(w_codes[1], w_scales[1], w_bf[1], cols)
-        for s in range(PACK):
+        round_w(vector, 1, pairs[0], every)
+        round_w(scalar, 1, pairs[1], slice(56, P))
+        round_w(vector, 1, pairs[1], slice(0, 56))
+        round_keys(scalar, 0, slice(416, 512))
+        for s in range(3):
+            round_queries(scalar, 0, s)
+        quantize_w(1, halves[0])
+        quantize_w(1, halves[1])
+        for s in range(3):
             query_passes(1, s, s)
-        round_queries(scalar, 1, 0)
-        round_queries(scalar, 1, 1)
-        round_queries(scalar, 1, 2)
+        query_passes(0, 3, 7)
+        query_passes(1, 3, 3)
+        for s in range(3):
+            round_queries(scalar, 1, s)
         round_queries(scalar, 0, 3)
         round_queries(scalar, 1, 3)
-        round_columns(vector, k_bf[0], k_f32[0], slice(KEYS_SECOND_END, J))
-        round_columns(vector, k_bf[1], k_f32[1], slice(KEYS_SCALAR_COLS, J))
+
+        round_keys(vector, 1, slice(0, J))
         quantize_keys(0, whole)
-        open_tile(0)
+        open_tile(0, 4)
         quantize_keys(1, whole)
-        store_planes()
-        close_tile(0)
-        both(1)
-        both(2)
-        fin(0)
-        open_tile(3)
-        close_tile(3)
-        fin(1)
-        fin(2)
-        fin(3)
+        store_key_words()
+        store_key_scales()
+        close_tile(0, 4)
+        both_spans(1, 5)
+        both_spans(2, 6)
+        finish(0, whole)
+        store_scores(slice(0, 1), whole)
+        open_tile(3, 7)
+        close_tile(3, 7)
+        finish(1, whole)
+        store_scores(slice(1, 2), whole)
+        finish(2, whole)
+        store_scores(slice(2, 3), whole)
+        finish(3, whole)
+        store_scores(slice(3, 4), whole)

@@ -39,7 +39,7 @@ def tile_mix_kvw_mask_kernel(tc, x, w, c, wk_words, wk_scales, msk, out_0, out_1
         ctx.enter_context(tc.manual_schedule())
 
         def new_tile(name, shape, dtype):
-            return sb.tile(shape, dtype, name=name, align_bytes=64)
+            return sb.tile(shape, dtype, name=name, align_bytes=256)
 
         def span_tiles(name, shape, dtype):
             return [new_tile("%s%d" % (name, a), shape, dtype) for a in range(D_SPANS)]
@@ -49,8 +49,9 @@ def tile_mix_kvw_mask_kernel(tc, x, w, c, wk_words, wk_scales, msk, out_0, out_1
 
         wk_words_raw = new_tile("wk_words_raw", [P, FP4_BYTES * D], U8)
         wk_scales_raw = new_tile("wk_scales_raw", [P, D], U8)
-        c_raw = new_tile("c_raw", [P, PACK, J], F32)
-        x_raw = new_tile("x_raw", [P, PACK, M], F32)
+        c_tile = new_tile("c_raw", [P, PACK, J], F32)
+        c_raw = [c_tile[:, :, cols] for cols in halves]
+        x_tile = new_tile("x_raw", [P, PACK, M], F32)
         w_tiles = span_tiles("w_raw", [P, PACK, SPAN], F32)
         w_raw = [tile[:] for tile in w_tiles]
         mask = new_tile("mask", [P, PACK, J], F32)
@@ -75,39 +76,42 @@ def tile_mix_kvw_mask_kernel(tc, x, w, c, wk_words, wk_scales, msk, out_0, out_1
         k_f32 = [k_all[:, a] for a in range(D_SPANS)]
         scores = new_tile("scores", [P, PACK, J], F32)
 
-        def deal(dealt, raw, a, groups):
+        def deal(copy, dealt, raw, a, groups):
             cols = slice(SPAN * a, SPAN * (a + 1))
-            nc.vector.tensor_copy(
+            copy(
                 out=dealt[:, cols].rearrange("p (r n) -> p r n", r=PACK)[:, groups, :],
                 in_=raw[:, cols].rearrange("p (n r) -> p r n", r=PACK)[:, groups, :],
             )
 
-        def deal_wk_words(a, groups):
-            deal(wk_dealt_words[:].bitcast(U16), wk_words_raw[:].bitcast(U16), a, groups)
+        def deal_wk_words(a, groups, copy=nc.vector.tensor_copy):
+            deal(copy, wk_dealt_words[:].bitcast(U16), wk_words_raw[:].bitcast(U16), a, groups)
 
         def deal_wk_scales(a, groups):
-            deal(wk_dealt_scales[:], wk_scales_raw[:], a, groups)
+            deal(nc.vector.tensor_copy, wk_dealt_scales[:], wk_scales_raw[:], a, groups)
 
-        def round_columns(copy, staged, raw, cols):
+        def round_columns(copy, staged, raw):
             copy(
-                out=staged[:, cols, :].rearrange("p (g i) t -> p g t i", i=PACK),
-                in_=raw[:, :, cols].rearrange("p t (g i) -> p g t i", i=PACK),
+                out=staged.rearrange("p (g i) t -> p g t i", i=PACK),
+                in_=raw.rearrange("p t (g i) -> p g t i", i=PACK),
             )
 
-        def round_dealt(copy, staged, raw, groups, ns):
-            copy(
-                out=staged.rearrange("p (r n) t -> p n t r", r=PACK)[:, ns, :, groups],
-                in_=raw.rearrange("p t (n r) -> p n t r", r=PACK)[:, ns, :, groups],
-            )
+        def round_c(copy, half, cols):
+            round_columns(copy, c_bf[:, halves[half], :][:, cols, :], c_raw[half][:, :, cols])
 
         def round_w(copy, a, groups, ns):
-            round_dealt(copy, w_bf[a][:], w_raw[a], groups, ns)
+            copy(
+                out=w_bf[a][:].rearrange("p (r n) t -> p n t r", r=PACK)[:, ns, :, groups],
+                in_=w_raw[a].rearrange("p t (n r) -> p n t r", r=PACK)[:, ns, :, groups],
+            )
 
         def round_keys(copy, a, cols):
-            round_columns(copy, k_bf[a], k_f32[a], cols)
+            round_columns(copy, k_bf[a][:, cols, :], k_f32[a][:, :, cols])
 
-        def round_x(copy, groups, ns):
-            round_dealt(copy, x_bf[:], x_raw[:], groups, ns)
+        def round_x(copy, ns):
+            copy(
+                out=x_bf[:].rearrange("p (r n) t -> p n t r", r=PACK)[:, ns],
+                in_=x_tile[:].rearrange("p t (n r) -> p n t r", r=PACK)[:, ns],
+            )
 
         def quantize(codes, scales, staged, cols):
             nc.vector.quantize_mx(
@@ -148,40 +152,19 @@ def tile_mix_kvw_mask_kernel(tc, x, w, c, wk_words, wk_scales, msk, out_0, out_1
             for i in range(2):
                 key_pass(acc[:, halves[i]], a, 2 * pair + i, halves[half])
 
-        def key_columns(number, copy, a, js):
-            acc = bank(number, "k_acc")
-            for r in range(PACK):
-                key_pass(acc[:, P * r : P * (r + 1)], a, r, js)
-            copy(out=k_f32[a][:, :, js], in_=acc[:].rearrange("p (r j) -> p r j", r=PACK))
-
-        def key_group(number, copy, a, r):
-            acc = bank(number, "k_acc")
-            key_pass(acc[:], a, r, whole)
-            copy(out=k_f32[a][:, r, :], in_=acc[:])
-
-        def warm_up(passes):
-            zeros = new_tile("zeros", [P, SPAN, PACK], BF16)
-            zero_codes = new_tile("zero_codes", [P, SPAN], U32)
-            zero_scales = new_tile("zero_scales", [P, SPAN], U8)
-            nc.vector.memset(zeros[:].rearrange("p n t -> p (n t)").bitcast(I32), 0)
-            quantize(zero_codes, zero_scales, zeros, whole)
-            acc = bank(7, "warm_acc")
-            for unused in range(passes):
-                nc.tensor.matmul_mx(
-                    out=acc[:],
-                    lhsT=zero_codes[:, 0:P].bitcast(FP8X4),
-                    lhsT_scale=zero_scales[:, 0:P],
-                    rhs=zero_codes[:].bitcast(FP8X4),
-                    rhs_scale=zero_scales[:],
-                    start=True,
-                    stop=True,
-                )
-
         def empty_keys(copy, a, half, pair):
             copy(
                 out=k_f32[a][:, 2 * pair : 2 * pair + 2, halves[half]],
                 in_=key_acc[a, half, pair][:].rearrange("p (i j) -> p i j", i=2),
             )
+
+        def key_group(number, a, r):
+            acc = bank(number, "k_acc")
+            key_acc[a, r] = acc
+            key_pass(acc[:], a, r, whole)
+
+        def empty_group(copy, a, r):
+            copy(out=k_f32[a][:, r, :], in_=key_acc[a, r][:])
 
         def store_keys():
             nc.sync.dma_start(out=out_1.rearrange("(a p r) j -> p a r j", a=D_SPANS, r=PACK), in_=k_all[:])
@@ -246,7 +229,7 @@ def tile_mix_kvw_mask_kernel(tc, x, w, c, wk_words, wk_scales, msk, out_0, out_1
                 stop=(a == D_SPANS - 1),
             )
 
-        def finish(s, js):
+        def finish(s, js=whole):
             nc.vector.scalar_tensor_tensor(
                 out=scores[:, s, js],
                 in0=score_acc[s][:, js],
@@ -256,21 +239,8 @@ def tile_mix_kvw_mask_kernel(tc, x, w, c, wk_words, wk_scales, msk, out_0, out_1
                 op1=ALU.add,
             )
 
-        def open_tile(s, number):
-            quantize_queries(s, 0, 1)
-            score_pass(s, 0, number)
-
-        def close_tile(s, number):
-            quantize_queries(s, 1, 1)
-            score_pass(s, 1, number)
-
-        def both_spans(s, number):
-            quantize_queries(s, 0, 2)
-            for a in range(D_SPANS):
-                score_pass(s, a, number)
-
-        def store_scores(tiles, js):
-            nc.sync.dma_start(out=out_0.rearrange("(p s) j -> p s j", s=PACK)[:, tiles, js], in_=scores[:, tiles, js])
+        def store_scores(s):
+            nc.sync.dma_start(out=out_0.rearrange("(p s) j -> p s j", s=PACK)[:, s, :], in_=scores[:, s, :])
 
         def load_mask():
             nc.sync.dma_start(out=mask[:], in_=msk.rearrange("(p s) j -> p s j", s=PACK))
@@ -294,33 +264,37 @@ def tile_mix_kvw_mask_kernel(tc, x, w, c, wk_words, wk_scales, msk, out_0, out_1
         all_groups = slice(0, PACK)
 
         nc.vector.memset(wk_scales_raw[:].bitcast(I32), 0)
-        load_rows(c_raw, c)
+        load_rows(c_tile, c)
         load_wk_scales()
         load_wk_words()
-        load_rows(x_raw, x)
-        for a in range(D_SPANS):
-            load_rows(w_tiles[a], w[:, a * SPAN : (a + 1) * SPAN])
+        load_rows(x_tile, x)
+        load_rows(w_tiles[0], w[:, 0:SPAN])
+        load_rows(w_tiles[1], w[:, SPAN:D])
         load_mask()
 
-
-        round_columns(vector, c_bf, c_raw, slice(0, 160))
-        round_columns(scalar, c_bf, c_raw, slice(160, HALF))
-        round_columns(scalar, c_bf, c_raw, halves[1])
+        round_c(vector, 0, slice(0, 160))
+        round_c(scalar, 0, slice(160, HALF))
+        round_c(scalar, 1, slice(0, HALF))
         deal_wk_scales(0, all_groups)
         quantize_c(halves[0])
         deal_wk_words(0, pairs[0])
         deal_wk_words(0, pairs[1])
+
         deal_wk_words(1, all_groups)
         quantize_c(halves[1])
         deal_wk_scales(1, all_groups)
-        for half in range(2):
-            for pair in range(2):
-                key_passes(2 * half + pair, 0, half, pair)
-                empty_keys(vector if (half, pair) == (2, 2) else scalar, 0, half, pair)
+        key_passes(0, 0, 0, 0)
+        empty_keys(scalar, 0, 0, 0)
+        key_passes(1, 0, 0, 1)
+        empty_keys(scalar, 0, 0, 1)
+        for pair in range(2):
+            key_passes(2 + pair, 0, 1, pair)
+            empty_keys(scalar, 0, 1, pair)
         for r in range(PACK):
-            key_group((PACK + r) % 4, scalar, 1, r)
+            key_group(r, 1, r)
+            empty_group(scalar, 1, r)
         store_keys()
-        round_x(vector, all_groups, every)
+        round_x(vector, every)
         round_keys(vector, 0, slice(0, 128))
         quantize_x(whole)
         round_w(vector, 0, pairs[0], every)
@@ -329,7 +303,6 @@ def tile_mix_kvw_mask_kernel(tc, x, w, c, wk_words, wk_scales, msk, out_0, out_1
         quantize_w(0, halves[1])
         round_keys(vector, 0, slice(128, 256))
         round_keys(scalar, 0, slice(256, 416))
-
         for s in range(3):
             query_passes(0, s, 4 + s)
         round_w(vector, 1, pairs[0], every)
@@ -349,22 +322,28 @@ def tile_mix_kvw_mask_kernel(tc, x, w, c, wk_words, wk_scales, msk, out_0, out_1
         round_queries(scalar, 0, 3)
         round_queries(scalar, 1, 3)
 
-        round_keys(vector, 1, slice(0, J))
+        round_keys(vector, 1, whole)
         quantize_keys(0, whole)
-        open_tile(0, 4)
+        quantize_queries(0, 0, 1)
+        score_pass(0, 0, 4)
         quantize_keys(1, whole)
-        store_key_words()
         store_key_scales()
-        close_tile(0, 4)
-        both_spans(1, 5)
-        both_spans(2, 6)
-        finish(0, whole)
-        store_scores(slice(0, 1), whole)
-        open_tile(3, 7)
-        close_tile(3, 7)
-        finish(1, whole)
-        store_scores(slice(1, 2), whole)
-        finish(2, whole)
-        store_scores(slice(2, 3), whole)
-        finish(3, whole)
-        store_scores(slice(3, 4), whole)
+        store_key_words()
+        quantize_queries(0, 1, 1)
+        score_pass(0, 1, 4)
+        quantize_queries(1, 0, 2)
+        score_pass(1, 0, 5)
+        score_pass(1, 1, 5)
+
+        quantize_queries(2, 0, 2)
+        score_pass(2, 0, 6)
+        score_pass(2, 1, 6)
+        finish(0)
+        store_scores(0)
+        quantize_queries(3, 0, 1)
+        score_pass(3, 0, 7)
+        quantize_queries(3, 1, 1)
+        score_pass(3, 1, 7)
+        for s in range(1, PACK):
+            finish(s)
+            store_scores(s)

@@ -49,8 +49,8 @@ def tile_mix_kvw_mask_kernel(tc, x, w, c, wk_words, wk_scales, msk, out_0, out_1
 
         wk_words_raw = new_tile("wk_words_raw", [P, FP4_BYTES * D], U8)
         wk_scales_raw = new_tile("wk_scales_raw", [P, D], U8)
-        c_tile = new_tile("c_raw", [P, PACK, J], F32)
-        c_raw = [c_tile[:, :, cols] for cols in halves]
+        c_tiles = span_tiles("c_raw", [P, PACK, HALF], F32)
+        c_raw = [tile[:] for tile in c_tiles]
         x_tile = new_tile("x_raw", [P, PACK, M], F32)
         w_tiles = span_tiles("w_raw", [P, PACK, SPAN], F32)
         w_raw = [tile[:] for tile in w_tiles]
@@ -158,14 +158,6 @@ def tile_mix_kvw_mask_kernel(tc, x, w, c, wk_words, wk_scales, msk, out_0, out_1
                 in_=key_acc[a, half, pair][:].rearrange("p (i j) -> p i j", i=2),
             )
 
-        def key_group(number, a, r):
-            acc = bank(number, "k_acc")
-            key_acc[a, r] = acc
-            key_pass(acc[:], a, r, whole)
-
-        def empty_group(copy, a, r):
-            copy(out=k_f32[a][:, r, :], in_=key_acc[a, r][:])
-
         def store_keys():
             nc.sync.dma_start(out=out_1.rearrange("(a p r) j -> p a r j", a=D_SPANS, r=PACK), in_=k_all[:])
 
@@ -239,8 +231,11 @@ def tile_mix_kvw_mask_kernel(tc, x, w, c, wk_words, wk_scales, msk, out_0, out_1
                 op1=ALU.add,
             )
 
-        def store_scores(s):
-            nc.sync.dma_start(out=out_0.rearrange("(p s) j -> p s j", s=PACK)[:, s, :], in_=scores[:, s, :])
+        def store_run(first, last):
+            nc.sync.dma_start(
+                out=out_0.rearrange("(p s) j -> p (s j)", s=PACK)[:, first:last],
+                in_=scores[:].rearrange("p s j -> p (s j)")[:, first:last],
+            )
 
         def load_mask():
             nc.sync.dma_start(out=mask[:], in_=msk.rearrange("(p s) j -> p s j", s=PACK))
@@ -264,9 +259,10 @@ def tile_mix_kvw_mask_kernel(tc, x, w, c, wk_words, wk_scales, msk, out_0, out_1
         all_groups = slice(0, PACK)
 
         nc.vector.memset(wk_scales_raw[:].bitcast(I32), 0)
-        load_rows(c_tile, c)
+        load_rows(c_tiles[0], c[:, halves[0]])
         load_wk_scales()
         load_wk_words()
+        load_rows(c_tiles[1], c[:, halves[1]])
         load_rows(x_tile, x)
         load_rows(w_tiles[0], w[:, 0:SPAN])
         load_rows(w_tiles[1], w[:, SPAN:D])
@@ -274,55 +270,55 @@ def tile_mix_kvw_mask_kernel(tc, x, w, c, wk_words, wk_scales, msk, out_0, out_1
 
         round_c(vector, 0, slice(0, 160))
         round_c(scalar, 0, slice(160, HALF))
-        round_c(scalar, 1, slice(0, HALF))
         deal_wk_scales(0, all_groups)
         quantize_c(halves[0])
         deal_wk_words(0, pairs[0])
         deal_wk_words(0, pairs[1])
-
-        deal_wk_words(1, all_groups)
-        quantize_c(halves[1])
         deal_wk_scales(1, all_groups)
-        key_passes(0, 0, 0, 0)
-        empty_keys(scalar, 0, 0, 0)
-        key_passes(1, 0, 0, 1)
-        empty_keys(scalar, 0, 0, 1)
-        for pair in range(2):
-            key_passes(2 + pair, 0, 1, pair)
-            empty_keys(scalar, 0, 1, pair)
-        for r in range(PACK):
-            key_group(r, 1, r)
-            empty_group(scalar, 1, r)
+        deal_wk_words(1, pairs[0])
+        round_c(vector, 1, slice(0, HALF))
+        deal_wk_words(1, pairs[1])
+        quantize_c(halves[1])
+        for half in range(2):
+            for a in range(D_SPANS):
+                for pair in range(2):
+                    key_passes((4 * half + 2 * a + pair) % 4, a, half, pair)
+                    empty_keys(scalar, a, half, pair)
         store_keys()
+        round_keys(vector, 0, slice(0, 96))
         round_x(vector, every)
-        round_keys(vector, 0, slice(0, 128))
+        round_keys(vector, 0, slice(96, 224))
         quantize_x(whole)
+
         round_w(vector, 0, pairs[0], every)
         round_w(vector, 0, pairs[1], every)
         quantize_w(0, halves[0])
         quantize_w(0, halves[1])
-        round_keys(vector, 0, slice(128, 256))
-        round_keys(scalar, 0, slice(256, 416))
+        round_keys(vector, 0, slice(224, 256))
+        round_keys(vector, 1, slice(0, 96))
+        round_keys(scalar, 1, slice(96, 256))
+        round_keys(scalar, 0, slice(256, 448))
         for s in range(3):
             query_passes(0, s, 4 + s)
+
         round_w(vector, 1, pairs[0], every)
         round_w(scalar, 1, pairs[1], slice(56, P))
         round_w(vector, 1, pairs[1], slice(0, 56))
-        round_keys(scalar, 0, slice(416, 512))
-        for s in range(3):
+        for s in range(0, 3):
             round_queries(scalar, 0, s)
         quantize_w(1, halves[0])
         quantize_w(1, halves[1])
         for s in range(3):
             query_passes(1, s, s)
+        round_queries(scalar, 1, 0)
         query_passes(0, 3, 7)
+        round_queries(scalar, 1, 1)
         query_passes(1, 3, 3)
-        for s in range(3):
-            round_queries(scalar, 1, s)
+        round_queries(scalar, 1, 2)
         round_queries(scalar, 0, 3)
         round_queries(scalar, 1, 3)
-
-        round_keys(vector, 1, whole)
+        round_keys(vector, 0, slice(448, 512))
+        round_keys(vector, 1, slice(256, 512))
         quantize_keys(0, whole)
         quantize_queries(0, 0, 1)
         score_pass(0, 0, 4)
@@ -334,16 +330,19 @@ def tile_mix_kvw_mask_kernel(tc, x, w, c, wk_words, wk_scales, msk, out_0, out_1
         quantize_queries(1, 0, 2)
         score_pass(1, 0, 5)
         score_pass(1, 1, 5)
-
         quantize_queries(2, 0, 2)
         score_pass(2, 0, 6)
         score_pass(2, 1, 6)
         finish(0)
-        store_scores(0)
         quantize_queries(3, 0, 1)
         score_pass(3, 0, 7)
+        finish(1, slice(0, 192))
+        store_run(0, 704)
         quantize_queries(3, 1, 1)
         score_pass(3, 1, 7)
-        for s in range(1, PACK):
-            finish(s)
-            store_scores(s)
+        finish(1, slice(192, J))
+        finish(2, slice(0, 320))
+        store_run(704, 1344)
+        finish(2, slice(320, J))
+        finish(3)
+        store_run(1344, PACK * J)

@@ -273,11 +273,10 @@ def tile_mix_kvw_mask_kernel(tc, x, w, c, wk_words, wk_scales, msk, out_0, out_1
         deal_wk_scales(0, all_groups)
         quantize_c(halves[0])
         deal_wk_words(0, pairs[0])
-        deal_wk_words(0, pairs[1])
+        deal_wk_words(0, pairs[1], scalar)
         deal_wk_scales(1, all_groups)
-        deal_wk_words(1, pairs[0])
+        deal_wk_words(1, all_groups, scalar)
         round_c(vector, 1, slice(0, HALF))
-        deal_wk_words(1, pairs[1])
         quantize_c(halves[1])
         for half in range(2):
             for a in range(D_SPANS):
@@ -285,19 +284,18 @@ def tile_mix_kvw_mask_kernel(tc, x, w, c, wk_words, wk_scales, msk, out_0, out_1
                     key_passes((4 * half + 2 * a + pair) % 4, a, half, pair)
                     empty_keys(scalar, a, half, pair)
         store_keys()
-        round_keys(vector, 0, slice(0, 96))
+        round_keys(vector, 0, slice(0, 128))
         round_x(vector, every)
-        round_keys(vector, 0, slice(96, 224))
+        round_keys(vector, 0, slice(128, 256))
         quantize_x(whole)
 
         round_w(vector, 0, pairs[0], every)
         round_w(vector, 0, pairs[1], every)
         quantize_w(0, halves[0])
         quantize_w(0, halves[1])
-        round_keys(vector, 0, slice(224, 256))
-        round_keys(vector, 1, slice(0, 96))
-        round_keys(scalar, 1, slice(96, 256))
-        round_keys(scalar, 0, slice(256, 448))
+        round_keys(vector, 0, slice(256, 384))
+        round_keys(scalar, 0, slice(384, 512))
+        round_keys(scalar, 1, slice(0, 224))
         for s in range(3):
             query_passes(0, s, 4 + s)
 
@@ -317,8 +315,7 @@ def tile_mix_kvw_mask_kernel(tc, x, w, c, wk_words, wk_scales, msk, out_0, out_1
         round_queries(scalar, 1, 2)
         round_queries(scalar, 0, 3)
         round_queries(scalar, 1, 3)
-        round_keys(vector, 0, slice(448, 512))
-        round_keys(vector, 1, slice(256, 512))
+        round_keys(vector, 1, slice(224, 512))
         quantize_keys(0, whole)
         quantize_queries(0, 0, 1)
         score_pass(0, 0, 4)
@@ -336,13 +333,12 @@ def tile_mix_kvw_mask_kernel(tc, x, w, c, wk_words, wk_scales, msk, out_0, out_1
         finish(0)
         quantize_queries(3, 0, 1)
         score_pass(3, 0, 7)
-        finish(1, slice(0, 192))
-        store_run(0, 704)
+        finish(1, slice(0, 256))
+        store_run(0, 768)
         quantize_queries(3, 1, 1)
         score_pass(3, 1, 7)
-        finish(1, slice(192, J))
-        finish(2, slice(0, 320))
-        store_run(704, 1344)
-        finish(2, slice(320, J))
+        finish(1, slice(256, J))
+        finish(2)
+        store_run(768, 1536)
         finish(3)
-        store_run(1344, PACK * J)
+        store_run(1536, PACK * J)

@@ -231,11 +231,8 @@ def tile_mix_kvw_mask_kernel(tc, x, w, c, wk_words, wk_scales, msk, out_0, out_1
                 op1=ALU.add,
             )
 
-        def store_run(first, last):
-            nc.sync.dma_start(
-                out=out_0.rearrange("(p s) j -> p (s j)", s=PACK)[:, first:last],
-                in_=scores[:].rearrange("p s j -> p (s j)")[:, first:last],
-            )
+        def store_scores(s):
+            nc.sync.dma_start(out=out_0.rearrange("(p s) j -> p s j", s=PACK)[:, s, :], in_=scores[:, s, :])
 
         def load_mask():
             nc.sync.dma_start(out=mask[:], in_=msk.rearrange("(p s) j -> p s j", s=PACK))
@@ -331,14 +328,11 @@ def tile_mix_kvw_mask_kernel(tc, x, w, c, wk_words, wk_scales, msk, out_0, out_1
         score_pass(2, 0, 6)
         score_pass(2, 1, 6)
         finish(0)
+        store_scores(0)
         quantize_queries(3, 0, 1)
         score_pass(3, 0, 7)
-        finish(1, slice(0, 256))
-        store_run(0, 768)
         quantize_queries(3, 1, 1)
         score_pass(3, 1, 7)
-        finish(1, slice(256, J))
-        finish(2)
-        store_run(768, 1536)
-        finish(3)
-        store_run(1536, PACK * J)
+        for s in range(1, PACK):
+            finish(s)
+            store_scores(s)

@@ -49,8 +49,7 @@ def tile_mix_kvw_mask_kernel(tc, x, w, c, wk_words, wk_scales, msk, out_0, out_1
 
         wk_words_raw = new_tile("wk_words_raw", [P, FP4_BYTES * D], U8)
         wk_scales_raw = new_tile("wk_scales_raw", [P, D], U8)
-        c_tiles = span_tiles("c_raw", [P, PACK, HALF], F32)
-        c_raw = [tile[:] for tile in c_tiles]
+        c_tile = new_tile("c_raw", [P, PACK, J], F32)
         x_tile = new_tile("x_raw", [P, PACK, M], F32)
         w_tiles = span_tiles("w_raw", [P, PACK, SPAN], F32)
         w_raw = [tile[:] for tile in w_tiles]
@@ -95,8 +94,8 @@ def tile_mix_kvw_mask_kernel(tc, x, w, c, wk_words, wk_scales, msk, out_0, out_1
                 in_=raw.rearrange("p t (g i) -> p g t i", i=PACK),
             )
 
-        def round_c(copy, half, cols):
-            round_columns(copy, c_bf[:, halves[half], :][:, cols, :], c_raw[half][:, :, cols])
+        def round_c(copy, cols):
+            round_columns(copy, c_bf[:, cols, :], c_tile[:, :, cols])
 
         def round_w(copy, a, groups, ns):
             copy(
@@ -240,6 +239,12 @@ def tile_mix_kvw_mask_kernel(tc, x, w, c, wk_words, wk_scales, msk, out_0, out_1
         def load_rows(raw, source):
             nc.sync.dma_start(out=raw[:], in_=source.rearrange("(p t) n -> p t n", t=PACK))
 
+        def load_c_runs(run):
+            nc.sync.dma_start(
+                out=c_tile[:].rearrange("p (u t) n -> p u (t n)", t=2)[:, :, run],
+                in_=c.rearrange("(p u t) n -> p u (t n)", p=P, t=2)[:, :, run],
+            )
+
         def load_wk_words():
             nc.sync.dma_start(out=wk_words_raw[:].bitcast(I32), in_=wk_words[0].bitcast(I32))
 
@@ -256,24 +261,24 @@ def tile_mix_kvw_mask_kernel(tc, x, w, c, wk_words, wk_scales, msk, out_0, out_1
         all_groups = slice(0, PACK)
 
         nc.vector.memset(wk_scales_raw[:].bitcast(I32), 0)
-        load_rows(c_tiles[0], c[:, halves[0]])
+        load_c_runs(slice(0, J + HALF))
         load_wk_scales()
         load_wk_words()
-        load_rows(c_tiles[1], c[:, halves[1]])
+        load_c_runs(slice(J + HALF, 2 * J))
         load_rows(x_tile, x)
         load_rows(w_tiles[0], w[:, 0:SPAN])
         load_rows(w_tiles[1], w[:, SPAN:D])
         load_mask()
 
-        round_c(vector, 0, slice(0, 160))
-        round_c(scalar, 0, slice(160, HALF))
+        round_c(vector, slice(0, 160))
+        round_c(scalar, slice(160, HALF))
         deal_wk_scales(0, all_groups)
         quantize_c(halves[0])
         deal_wk_words(0, pairs[0])
         deal_wk_words(0, pairs[1], scalar)
         deal_wk_scales(1, all_groups)
         deal_wk_words(1, all_groups, scalar)
-        round_c(vector, 1, slice(0, HALF))
+        round_c(vector, halves[1])
         quantize_c(halves[1])
         for half in range(2):
             for a in range(D_SPANS):
@@ -281,24 +286,21 @@ def tile_mix_kvw_mask_kernel(tc, x, w, c, wk_words, wk_scales, msk, out_0, out_1
                     key_passes((4 * half + 2 * a + pair) % 4, a, half, pair)
                     empty_keys(scalar, a, half, pair)
         store_keys()
-        round_keys(vector, 0, slice(0, 128))
         round_x(vector, every)
-        round_keys(vector, 0, slice(128, 256))
+        round_keys(vector, 0, slice(0, 192))
         quantize_x(whole)
-
         round_w(vector, 0, pairs[0], every)
         round_w(vector, 0, pairs[1], every)
         quantize_w(0, halves[0])
         quantize_w(0, halves[1])
-        round_keys(vector, 0, slice(256, 384))
+        round_keys(vector, 0, slice(192, 384))
         round_keys(scalar, 0, slice(384, 512))
-        round_keys(scalar, 1, slice(0, 224))
+        round_keys(scalar, 1, slice(0, 160))
         for s in range(3):
             query_passes(0, s, 4 + s)
-
         round_w(vector, 1, pairs[0], every)
-        round_w(scalar, 1, pairs[1], slice(56, P))
-        round_w(vector, 1, pairs[1], slice(0, 56))
+        round_w(scalar, 1, pairs[1], slice(52, P))
+        round_w(vector, 1, pairs[1], slice(0, 52))
         for s in range(0, 3):
             round_queries(scalar, 0, s)
         quantize_w(1, halves[0])
@@ -312,7 +314,7 @@ def tile_mix_kvw_mask_kernel(tc, x, w, c, wk_words, wk_scales, msk, out_0, out_1
         round_queries(scalar, 1, 2)
         round_queries(scalar, 0, 3)
         round_queries(scalar, 1, 3)
-        round_keys(vector, 1, slice(224, 512))
+        round_keys(vector, 1, slice(160, 512))
         quantize_keys(0, whole)
         quantize_queries(0, 0, 1)
         score_pass(0, 0, 4)

@@ -26,6 +26,7 @@ SCALE_ROWS = 4
 FP4_BYTES = 2
 SCORE_SCALE = 0.03125
 KEY_SCALE_ROW = 4
+KEY_BANKS = (0, 1, 2, 3, 7, 0, 1, 2)
 
 
 def tile_mix_kvw_mask_kernel(tc, x, w, c, wk_words, wk_scales, msk, out_0, out_1, out_2, out_3):
@@ -274,8 +275,8 @@ def tile_mix_kvw_mask_kernel(tc, x, w, c, wk_words, wk_scales, msk, out_0, out_1
         round_c(scalar, slice(160, HALF))
         deal_wk_scales(0, all_groups)
         quantize_c(halves[0])
-        deal_wk_words(0, pairs[0])
-        deal_wk_words(0, pairs[1], scalar)
+        deal_wk_words(0, pairs[0], scalar)
+        deal_wk_words(0, pairs[1])
         deal_wk_scales(1, all_groups)
         deal_wk_words(1, all_groups, scalar)
         round_c(vector, halves[1])
@@ -283,7 +284,7 @@ def tile_mix_kvw_mask_kernel(tc, x, w, c, wk_words, wk_scales, msk, out_0, out_1
         for half in range(2):
             for a in range(D_SPANS):
                 for pair in range(2):
-                    key_passes((4 * half + 2 * a + pair) % 4, a, half, pair)
+                    key_passes(KEY_BANKS[4 * half + 2 * a + pair], a, half, pair)
                     empty_keys(scalar, a, half, pair)
         store_keys()
         round_x(vector, every)
@@ -295,7 +296,7 @@ def tile_mix_kvw_mask_kernel(tc, x, w, c, wk_words, wk_scales, msk, out_0, out_1
         quantize_w(0, halves[1])
         round_keys(vector, 0, slice(192, 384))
         round_keys(scalar, 0, slice(384, 512))
-        round_keys(scalar, 1, slice(0, 160))
+        round_keys(scalar, 1, slice(0, 208))
         for s in range(3):
             query_passes(0, s, 4 + s)
         round_w(vector, 1, pairs[0], every)
@@ -314,7 +315,7 @@ def tile_mix_kvw_mask_kernel(tc, x, w, c, wk_words, wk_scales, msk, out_0, out_1
         round_queries(scalar, 1, 2)
         round_queries(scalar, 0, 3)
         round_queries(scalar, 1, 3)
-        round_keys(vector, 1, slice(160, 512))
+        round_keys(vector, 1, slice(208, 512))
         quantize_keys(0, whole)
         quantize_queries(0, 0, 1)
         score_pass(0, 0, 4)

@@ -296,7 +296,7 @@ def tile_mix_kvw_mask_kernel(tc, x, w, c, wk_words, wk_scales, msk, out_0, out_1
         quantize_w(0, halves[1])
         round_keys(vector, 0, slice(192, 384))
         round_keys(scalar, 0, slice(384, 512))
-        round_keys(scalar, 1, slice(0, 208))
+        round_keys(scalar, 1, slice(0, 192))
         for s in range(3):
             query_passes(0, s, 4 + s)
         round_w(vector, 1, pairs[0], every)
@@ -315,7 +315,7 @@ def tile_mix_kvw_mask_kernel(tc, x, w, c, wk_words, wk_scales, msk, out_0, out_1
         round_queries(scalar, 1, 2)
         round_queries(scalar, 0, 3)
         round_queries(scalar, 1, 3)
-        round_keys(vector, 1, slice(208, 512))
+        round_keys(vector, 1, slice(192, 512))
         quantize_keys(0, whole)
         quantize_queries(0, 0, 1)
         score_pass(0, 0, 4)

from contextlib import ExitStack

import concourse.mybir as mybir

K, D, M, J = 512, 1024, 512, 512
FLOPS = 2 * K * D * M + 2 * K * D * J + 2 * D * M * J

F32 = mybir.dt.float32
BF16 = mybir.dt.bfloat16
I32 = mybir.dt.int32
U32 = mybir.dt.uint32
U16 = mybir.dt.uint16
U8 = mybir.dt.uint8
FP8X4 = mybir.dt.float8_e4m3fn_x4
FP4X4 = mybir.dt.float4_e2m1fn_x4
ALU = mybir.AluOpType

P = 128
PACK = 4
SPAN = P * PACK
HALF = SPAN // 2
D_SPANS = D // SPAN
BLOCK = 32
QUADRANT = 32
SCALE_ROWS = 4
FP4_BYTES = 2
SCORE_SCALE = 0.03125
KEY_SCALE_ROW = 4
KEY_BANKS = (0, 1, 2, 3, 7, 0, 1, 2)


def tile_mix_kvw_mask_kernel(tc, x, w, c, wk_words, wk_scales, msk, out_0, out_1, out_2, out_3):
    nc = tc.nc
    halves = [slice(0, HALF), slice(HALF, SPAN)]
    whole = slice(0, SPAN)

    with ExitStack() as ctx:
        sb = ctx.enter_context(tc.tile_pool(name="sb", bufs=1))
        psum = ctx.enter_context(tc.psum_pool(name="psum", bufs=1))
        ctx.enter_context(tc.manual_schedule())

        def new_tile(name, shape, dtype):
            return sb.tile(shape, dtype, name=name, align_bytes=256)

        def span_tiles(name, shape, dtype):
            return [new_tile("%s%d" % (name, a), shape, dtype) for a in range(D_SPANS)]

        def bank(number, name):
            return psum.tile([P, SPAN], F32, tag="bank%d" % number, name=name)

        wk_words_raw = new_tile("wk_words_raw", [P, FP4_BYTES * D], U8)
        wk_scales_raw = new_tile("wk_scales_raw", [P, D], U8)
        c_tile = new_tile("c_raw", [P, PACK, J], F32)
        x_tile = new_tile("x_raw", [P, PACK, M], F32)
        w_tiles = span_tiles("w_raw", [P, PACK, SPAN], F32)
        w_raw = [tile[:] for tile in w_tiles]
        mask = new_tile("mask", [P, PACK, J], F32)
        c_bf = new_tile("c_bf", [P, J, PACK], BF16)
        x_bf = new_tile("x_bf", [P, M, PACK], BF16)
        w_bf = span_tiles("w_bf", [P, SPAN, PACK], BF16)
        k_bf = span_tiles("k_bf", [P, J, PACK], BF16)
        q_bf = new_tile("q_bf", [P, D_SPANS * M, PACK], BF16)
        wk_dealt_words = new_tile("wk_dealt_words", [P, FP4_BYTES * D], U8)
        wk_dealt_scales = new_tile("wk_dealt_scales", [P, D], U8)
        c_codes = new_tile("c_codes", [P, J], U32)
        c_scales = new_tile("c_scales", [P, J], U8)
        x_codes = new_tile("x_codes", [P, M], U32)
        x_scales = new_tile("x_scales", [P, M], U8)
        w_codes = span_tiles("w_codes", [P, SPAN], U32)
        w_scales = span_tiles("w_scales", [P, SPAN], U8)
        q_codes = new_tile("q_codes", [P, D_SPANS * M], U32)
        q_scales = new_tile("q_scales", [P, D_SPANS * M], U8)
        k_codes = new_tile("k_codes", [P, D_SPANS, J], U32)
        k_scales = new_tile("k_scales", [P, D_SPANS, J], U8)
        k_all = new_tile("k_f32", [P, D_SPANS, PACK, J], F32)
        k_f32 = [k_all[:, a] for a in range(D_SPANS)]
        scores = new_tile("scores", [P, PACK, J], F32)

        def deal(copy, dealt, raw, a, groups):
            cols = slice(SPAN * a, SPAN * (a + 1))
            copy(
                out=dealt[:, cols].rearrange("p (r n) -> p r n", r=PACK)[:, groups, :],
                in_=raw[:, cols].rearrange("p (n r) -> p r n", r=PACK)[:, groups, :],
            )

        def deal_wk_words(a, groups, copy=nc.vector.tensor_copy):
            deal(copy, wk_dealt_words[:].bitcast(U16), wk_words_raw[:].bitcast(U16), a, groups)

        def deal_wk_scales(a, groups):
            deal(nc.vector.tensor_copy, wk_dealt_scales[:], wk_scales_raw[:], a, groups)

        def round_columns(copy, staged, raw):
            copy(
                out=staged.rearrange("p (g i) t -> p g t i", i=PACK),
                in_=raw.rearrange("p t (g i) -> p g t i", i=PACK),
            )

        def round_c(copy, cols):
            round_columns(copy, c_bf[:, cols, :], c_tile[:, :, cols])

        def round_w(copy, a, groups, ns):
            copy(
                out=w_bf[a][:].rearrange("p (r n) t -> p n t r", r=PACK)[:, ns, :, groups],
                in_=w_raw[a].rearrange("p t (n r) -> p n t r", r=PACK)[:, ns, :, groups],
            )

        def round_keys(copy, a, cols):
            round_columns(copy, k_bf[a][:, cols, :], k_f32[a][:, :, cols])

        def round_x(copy, ns):
            copy(
                out=x_bf[:].rearrange("p (r n) t -> p n t r", r=PACK)[:, ns],
                in_=x_tile[:].rearrange("p t (n r) -> p n t r", r=PACK)[:, ns],
            )

        def quantize(codes, scales, staged, cols):
            nc.vector.quantize_mx(
                out=codes[:, cols].bitcast(FP8X4),
                scales=scales[:, cols],
                in_=staged[:, cols, :].rearrange("p n t -> p (n t)"),
            )

        def quantize_keys(a, cols):
            quantize(k_codes[:, a, :], k_scales[KEY_SCALE_ROW:P, a, :], k_bf[a], cols)

        def quantize_c(cols):
            quantize(c_codes, c_scales, c_bf, cols)

        def quantize_x(cols):
            quantize(x_codes, x_scales, x_bf, cols)

        def quantize_w(a, cols):
            quantize(w_codes[a], w_scales[a], w_bf[a], cols)

        def key_pass(out, a, r, js):
            col = SPAN * a + P * r
            nc.tensor.matmul_mx(
                out=out,
                lhsT=wk_dealt_words[:, FP4_BYTES * col : FP4_BYTES * (col + P)].bitcast(FP4X4),
                lhsT_scale=wk_dealt_scales[:, col : col + P],
                rhs=c_codes[:, js].bitcast(FP8X4),
                rhs_scale=c_scales[:, js],
                start=True,
                stop=True,
            )

        key_acc = {}

        def key_passes(number, a, half, pair):
            acc = bank(number, "k_acc")
            key_acc[a, half, pair] = acc
            for i in range(2):
                key_pass(acc[:, halves[i]], a, 2 * pair + i, halves[half])

        def empty_keys(copy, a, half, pair):
            copy(
                out=k_f32[a][:, 2 * pair : 2 * pair + 2, halves[half]],
                in_=key_acc[a, half, pair][:].rearrange("p (i j) -> p i j", i=2),
            )

        def store_keys():
            nc.sync.dma_start(out=out_1.rearrange("(a p r) j -> p a r j", a=D_SPANS, r=PACK), in_=k_all[:])

        def store_key_words():
            nc.sync.dma_start(
                out=out_2.rearrange("a p j i -> p a (j i)").bitcast(I32),
                in_=k_codes[:].bitcast(I32),
            )

        def store_key_scales():
            for row in range(SCALE_ROWS):
                nc.sync.dma_start(
                    out=out_3[:, row : P * PACK // BLOCK : SCALE_ROWS, :].rearrange("a q j -> q a j").bitcast(I32),
                    in_=k_scales[KEY_SCALE_ROW + row : P : QUADRANT, :, :].bitcast(I32),
                )

        def query_cols(s, a, spans):
            first = P * (D_SPANS * s + a)
            return slice(first, first + P * spans)

        query_acc = {}

        def query_passes(a, s, number):
            acc = bank(number, "q_acc")
            query_acc[a, s] = acc
            ms = slice(P * s, P * (s + 1))
            for r in range(PACK):
                group = slice(P * r, P * (r + 1))
                nc.tensor.matmul_mx(
                    out=acc[:, group],
                    lhsT=w_codes[a][:, group].bitcast(FP8X4),
                    lhsT_scale=w_scales[a][:, group],
                    rhs=x_codes[:, ms].bitcast(FP8X4),
                    rhs_scale=x_scales[:, ms],
                    start=True,
                    stop=True,
                )

        def round_queries(copy, a, s):
            copy(
                out=q_bf[:, query_cols(s, a, 1), :],
                in_=query_acc[a, s][:].rearrange("p (r n) -> p n r", r=PACK),
            )

        def quantize_queries(s, a, spans):
            quantize(q_codes, q_scales, q_bf, query_cols(s, a, spans))

        score_acc = {}

        def score_pass(s, a, number):
            if a == 0:
                score_acc[s] = bank(number, "s_acc")
            cols = query_cols(s, a, 1)
            nc.tensor.matmul_mx(
                out=score_acc[s][:],
                lhsT=q_codes[:, cols].bitcast(FP8X4),
                lhsT_scale=q_scales[:, cols],
                rhs=k_codes[:, a, :].bitcast(FP8X4),
                rhs_scale=k_scales[KEY_SCALE_ROW:P, a, :],
                start=(a == 0),
                stop=(a == D_SPANS - 1),
            )

        def finish(s, js=whole):
            nc.vector.scalar_tensor_tensor(
                out=scores[:, s, js],
                in0=score_acc[s][:, js],
                scalar=SCORE_SCALE,
                in1=mask[:, s, js],
                op0=ALU.mult,
                op1=ALU.add,
            )

        def store_scores(s):
            nc.sync.dma_start(out=out_0.rearrange("(p s) j -> p s j", s=PACK)[:, s, :], in_=scores[:, s, :])

        def load_mask():
            nc.sync.dma_start(out=mask[:], in_=msk.rearrange("(p s) j -> p s j", s=PACK))

        def load_rows(raw, source):
            nc.sync.dma_start(out=raw[:], in_=source.rearrange("(p t) n -> p t n", t=PACK))

        def load_c_runs(run):
            nc.sync.dma_start(
                out=c_tile[:].rearrange("p (u t) n -> p u (t n)", t=2)[:, :, run],
                in_=c.rearrange("(p u t) n -> p u (t n)", p=P, t=2)[:, :, run],
            )

        def load_wk_words():
            nc.sync.dma_start(out=wk_words_raw[:].bitcast(I32), in_=wk_words[0].bitcast(I32))

        def load_wk_scales():
            for row in range(SCALE_ROWS):
                nc.sync.dma_start(
                    out=wk_scales_raw[row:P:QUADRANT, :].bitcast(I32),
                    in_=wk_scales[0, row : P * PACK // BLOCK : SCALE_ROWS, :].bitcast(I32),
                )

        vector, scalar = nc.vector.tensor_copy, nc.scalar.copy
        every = slice(0, P)
        pairs = [slice(0, 2), slice(2, PACK)]
        all_groups = slice(0, PACK)

        nc.vector.memset(wk_scales_raw[:].bitcast(I32), 0)
        load_c_runs(slice(0, J + HALF))
        load_wk_scales()
        load_wk_words()
        load_c_runs(slice(J + HALF, 2 * J))
        load_rows(x_tile, x)
        load_rows(w_tiles[0], w[:, 0:SPAN])
        load_rows(w_tiles[1], w[:, SPAN:D])
        load_mask()

        round_c(vector, slice(0, 160))
        round_c(scalar, slice(160, HALF))
        deal_wk_scales(0, all_groups)
        quantize_c(halves[0])
        deal_wk_words(0, pairs[0], scalar)
        deal_wk_words(0, pairs[1])
        deal_wk_scales(1, all_groups)
        deal_wk_words(1, all_groups, scalar)
        round_c(vector, halves[1])
        quantize_c(halves[1])
        for half in range(2):
            for a in range(D_SPANS):
                for pair in range(2):
                    key_passes(KEY_BANKS[4 * half + 2 * a + pair], a, half, pair)
                    empty_keys(scalar, a, half, pair)
        store_keys()
        round_x(vector, every)
        round_keys(vector, 0, slice(0, 192))
        quantize_x(whole)
        round_w(vector, 0, pairs[0], every)
        round_w(vector, 0, pairs[1], every)
        quantize_w(0, halves[0])
        quantize_w(0, halves[1])
        round_keys(vector, 0, slice(192, 384))
        round_keys(scalar, 0, slice(384, 512))
        round_keys(scalar, 1, slice(0, 192))
        for s in range(3):
            query_passes(0, s, 4 + s)
        round_w(vector, 1, pairs[0], every)
        round_w(scalar, 1, pairs[1], slice(52, P))
        round_w(vector, 1, pairs[1], slice(0, 52))
        for s in range(0, 3):
            round_queries(scalar, 0, s)
        quantize_w(1, halves[0])
        quantize_w(1, halves[1])
        for s in range(3):
            query_passes(1, s, s)
        round_queries(scalar, 1, 0)
        query_passes(0, 3, 7)
        round_queries(scalar, 1, 1)
        query_passes(1, 3, 3)
        round_queries(scalar, 1, 2)
        round_queries(scalar, 0, 3)
        round_queries(scalar, 1, 3)
        round_keys(vector, 1, slice(192, 512))
        quantize_keys(0, whole)
        quantize_queries(0, 0, 1)
        score_pass(0, 0, 4)
        quantize_keys(1, whole)
        store_key_scales()
        store_key_words()
        quantize_queries(0, 1, 1)
        score_pass(0, 1, 4)
        quantize_queries(1, 0, 2)
        score_pass(1, 0, 5)
        score_pass(1, 1, 5)
        quantize_queries(2, 0, 2)
        score_pass(2, 0, 6)
        score_pass(2, 1, 6)
        finish(0)
        store_scores(0)
        quantize_queries(3, 0, 1)
        score_pass(3, 0, 7)
        quantize_queries(3, 1, 1)
        score_pass(3, 1, 7)
        for s in range(1, PACK):
            finish(s)
            store_scores(s)
